import numpy as np
import ml_dtypes


def mxq(x, axis, fmt="e4m3"):
    dtype, down = {"e4m3": (ml_dtypes.float8_e4m3fn, 7), "e5m2": (ml_dtypes.float8_e5m2, 14)}[fmt]
    v = np.moveaxis(np.asarray(x, np.float32).astype(ml_dtypes.bfloat16).astype(np.float64), axis, -1)
    blocks = v.reshape(v.shape[:-1] + (-1, 32))
    amax = np.abs(blocks).max(-1, keepdims=True)
    byte = np.maximum(np.where(amax > 0, np.frexp(amax)[1] - 1 + 127, 0) - down, 1)
    scale = np.exp2(byte - 127.0)
    codes = (blocks / scale).astype(np.float32).astype(dtype).astype(np.float64)
    return np.moveaxis((codes * scale).reshape(v.shape), -1, axis)


WIDE = False


def mx_kscale(k):
    if not WIDE:
        return np.ones(k)
    levels = np.array([10, -10, 5, -5, 0])
    if k % 512:
        return np.exp2(np.random.permutation(np.resize(levels, k // 32))).repeat(32)
    a = np.empty((k // 512, 16))
    for p in range(k // 512):
        a[p, :8] = np.random.permutation(np.resize(levels, 8))
        for g in range(8):
            far = levels[np.abs(levels - a[p, g]) >= 10]
            a[p, g + 8] = far[np.random.randint(len(far))]
    return np.exp2(a.ravel()).repeat(32)


def f64(x):
    return np.asarray(x).astype(np.float64)


def striped(idx):
    return np.tile(idx.reshape(-1, 16).T, (8, 1)).astype(np.uint16)


def unstriped(offs):
    return offs[:16].T.reshape(-1).astype(np.int64)


E2M1 = np.array([0.0, 0.5, 1.0, 1.5, 2.0, 3.0, 4.0, 6.0, -0.0, -0.5, -1.0, -1.5, -2.0, -3.0, -4.0, -6.0])


def pack_weight(w, fmt):
    k, n = w.shape
    w = f64(np.asarray(w, np.float32).astype(ml_dtypes.bfloat16)).reshape(k // 32, 32, n)
    amax = np.abs(w).max(1)
    if fmt == "e4m3":
        byte = np.frexp(amax)[1] - 1 + 127 - 7
    else:
        mant, ex = np.frexp(amax / 6.0)
        byte = np.where(mant > 0.5, ex, ex - 1) + 127
    byte = np.clip(np.where(amax > 0, byte, 1), 1, 254)
    scaled = (w * np.exp2(127.0 - byte)[:, None, :]).reshape(k, n).astype(np.float32)
    by_word = np.ascontiguousarray(scaled.reshape(k // 512, 128, 4, n).transpose(0, 1, 3, 2))
    if fmt == "e4m3":
        words = by_word.astype(ml_dtypes.float8_e4m3fn).view(np.uint8)
    else:
        c = by_word.astype(ml_dtypes.float4_e2m1fn).view(np.uint8) & 0xF
        words = (c[..., 0::2] | (c[..., 1::2] << 4)).reshape(k // 512, 128, 2 * n)
    return np.ascontiguousarray(words), np.ascontiguousarray(byte.astype(np.uint8).reshape(k // 512, 16, n))


def unpack_weight(words, scales, fmt):
    g, _, n = scales.shape
    words = np.ascontiguousarray(words).reshape(g, 128, n, -1)
    if fmt == "e4m3":
        vals = words.view(ml_dtypes.float8_e4m3fn).astype(np.float64)
    else:
        nib = np.empty((g, 128, n, 4), np.uint8)
        nib[..., 0::2] = words & 0xF
        nib[..., 1::2] = words >> 4
        vals = E2M1[nib]
    vals = vals * np.repeat(np.exp2(scales.astype(np.float64) - 127.0), 8, axis=1)[..., None]
    return vals.transpose(0, 1, 3, 2).reshape(g * 512, n)


def relu(v):
    return np.maximum(v, 0.0)


K, T, E, C, H, N = 512, 1024, 4, 128, 1024, 128


def by_expert(wq, xq):
    return np.concatenate([wq[e].T @ xq[:, e * C:(e + 1) * C] for e in range(E)], axis=1)


def setup_inputs():
    n = np.random.standard_normal
    s = mx_kscale(K)[:, None]
    u = mx_kscale(H)
    w1 = [pack_weight(m, "e2m1") for m in n((E, K, H)) / np.sqrt(K) / s[None]]
    w3 = [pack_weight(m, "e2m1") for m in n((E, K, H)) / np.sqrt(K) / s[None] * u[None, None, :]]
    w2 = [pack_weight(m, "e2m1") for m in n((E, H, N)) / np.sqrt(H) / u[None, :, None]]
    return {
        "xT": (n((K, T)) * s).astype(np.float32),
        "w1_words": np.stack([m[0] for m in w1]),
        "w1_scales": np.stack([m[1] for m in w1]),
        "w3_words": np.stack([m[0] for m in w3]),
        "w3_scales": np.stack([m[1] for m in w3]),
        "w2_words": np.stack([m[0] for m in w2]),
        "w2_scales": np.stack([m[1] for m in w2]),
        "gate": np.tile(np.random.uniform(0.2, 1.0, E * C), (N, 1)).astype(np.float32),
        "offs": striped(np.random.permutation(T)[:E * C]),
        "dst": striped(np.random.permutation(T)[:E * C]),
    }


def reference(xT, w1_words, w1_scales, w3_words, w3_scales, w2_words, w2_scales, gate, offs, dst):
    idx = unstriped(offs)
    w1 = np.stack([unpack_weight(w1_words[e], w1_scales[e], "e2m1") for e in range(E)])
    w3 = np.stack([unpack_weight(w3_words[e], w3_scales[e], "e2m1") for e in range(E)])
    w2 = np.stack([unpack_weight(w2_words[e], w2_scales[e], "e2m1") for e in range(E)])
    xq = mxq(f64(xT)[:, idx], 0, "e4m3")
    h = relu(by_expert(w1, xq))
    h = h * by_expert(w3, xq)
    y = by_expert(w2, mxq(h, 0, "e4m3"))
    out = np.zeros((N, T))
    out[:, unstriped(dst)] = f64(gate) * y
    return out

@@ -1,0 +1,228 @@
+from contextlib import ExitStack
+
+import concourse.mybir as mybir
+from concourse.masks import make_identity
+
+K, T, E, C, H, N = 512, 1024, 4, 128, 1024, 128
+P = 128
+FLOPS = 2 * E * C * (2 * K * H + H * N)
+
+F32 = mybir.dt.float32
+BF16 = mybir.dt.bfloat16
+I32 = mybir.dt.int32
+U32 = mybir.dt.uint32
+U16 = mybir.dt.uint16
+U8 = mybir.dt.uint8
+FP8X4 = mybir.dt.float8_e4m3fn_x4
+FP4X4 = mybir.dt.float4_e2m1fn_x4
+MULT = mybir.AluOpType.mult
+RELU = mybir.ActivationFunctionType.Relu
+COPY = mybir.ActivationFunctionType.Copy
+
+PACK = 4
+HALF = 512
+PASSES = H // HALF
+SCALE_ROWS = 16
+LIST_COLS = C // 16
+
+
+def tile_moe_two_glu_relu_kernel(
+    tc, xT, w1_words, w1_scales, w3_words, w3_scales, w2_words, w2_scales, gate, offs, dst, out
+):
+    nc = tc.nc
+    with ExitStack() as ctx:
+        keep = ctx.enter_context(tc.tile_pool(name="keep", bufs=1))
+        work = ctx.enter_context(tc.tile_pool(name="work", bufs=4))
+        psum_first = ctx.enter_context(tc.psum_pool(name="psum_first", bufs=2))
+        psum_turned = ctx.enter_context(tc.psum_pool(name="psum_turned", bufs=2))
+        psum_second = ctx.enter_context(tc.psum_pool(name="psum_second", bufs=2))
+
+        sources = keep.tile([P, E * LIST_COLS], U16, name="sources")
+        places = keep.tile([P, E * LIST_COLS], U16, name="places")
+        planes = [keep.tile([P, T], F32, name="plane%d" % t) for t in range(PACK)]
+        gates = keep.tile([P, E * C], F32, name="gates")
+        w1 = [keep.tile([P, 2 * H], U8, name="w1_%d" % e, align_bytes=64) for e in range(E)]
+        w3 = [keep.tile([P, 2 * H], U8, name="w3_%d" % e, align_bytes=64) for e in range(E)]
+        w2 = keep.tile([P, E * PASSES, 2 * N], U8, name="w2", align_bytes=64)
+        s1 = keep.tile([P, E, H], U8, name="s1", align_bytes=64)
+        s3 = keep.tile([P, E, H], U8, name="s3", align_bytes=64)
+        s2 = keep.tile([P, E * PASSES, N], U8, name="s2", align_bytes=64)
+        identity = keep.tile([P, P], F32, name="identity")
+        result = keep.tile([P, T], F32, name="result")
+
+        column = keep.tile([P, 1], F32, name="column")
+        nc.gpsimd.memset(column[:], 0.0)
+        nc.scalar.activation(column[:], column[:], RELU)
+        for scales in (s1, s3, s2):
+            nc.vector.memset(scales[:].bitcast(I32), 0)
+        make_identity(nc, identity[:])
+        nc.gpsimd.memset(result[:], 0.0)
+
+        def load_plane(t):
+            nc.sync.dma_start(planes[t][:], xT.rearrange("(p t) n -> p t n", t=PACK)[:, t, :])
+
+        def load_words(tiles, words, e):
+            nc.sync.dma_start(tiles[e][:].bitcast(I32), words[e, 0].bitcast(I32))
+
+        def load_scales(queue, tile, rows):
+            for r in range(4):
+                queue.dma_start(tile[:].bitcast(I32)[r:P:32, :, :], rows[:, r:SCALE_ROWS:4, :].rearrange("m q c -> q m c"))
+
+        load_plane(0)
+        nc.sync.dma_start(sources[:], offs)
+        load_plane(1)
+        load_plane(2)
+        load_plane(3)
+        load_scales(nc.sync, s1, w1_scales.bitcast(I32).rearrange("e s q i -> (e s) q i"))
+        load_words(w1, w1_words, 0)
+        load_scales(nc.sync, s3, w3_scales.bitcast(I32).rearrange("e s q i -> (e s) q i"))
+        load_words(w3, w3_words, 0)
+        load_words(w1, w1_words, 1)
+        load_words(w3, w3_words, 1)
+        load_scales(nc.gpsimd, s2, w2_scales.bitcast(I32).rearrange("e s q n -> (e s) q n"))
+        nc.sync.dma_start(w2[:].bitcast(I32), w2_words.bitcast(I32).rearrange("e s p c -> p (e s) c"))
+        load_words(w1, w1_words, 2)
+        load_words(w3, w3_words, 2)
+        nc.sync.dma_start(places[:], dst)
+        load_words(w1, w1_words, 3)
+        load_words(w3, w3_words, 3)
+        nc.sync.dma_start(gates[:], gate)
+
+        rounded = [keep.tile([P, T], BF16, name="rounded%d" % t, align_bytes=64) for t in range(2)]
+        tokens = [keep.tile([P, C, PACK], BF16, name="tokens%d" % e, align_bytes=64) for e in range(E)]
+        token_codes = [keep.tile([P, C], U32, name="token_codes%d" % e, align_bytes=64) for e in range(E)]
+        token_scales = [keep.tile([P, C], U8, name="token_scales%d" % e, align_bytes=64) for e in range(E)]
+
+        def slots_of(offsets, e):
+            return offsets[:, e * LIST_COLS : (e + 1) * LIST_COLS]
+
+        def pick(e, t):
+            if t < 2:
+                nc.scalar.activation(tokens[e][:, :, t], rounded[t][:].indirect(slots_of(sources, e)), COPY)
+            else:
+                nc.vector.tensor_copy(tokens[e][:, :, t], planes[t][:].indirect(slots_of(sources, e)))
+
+        def quantise_tokens(e):
+            nc.vector.quantize_mx(
+                out=token_codes[e][:].bitcast(FP8X4),
+                scales=token_scales[e][:],
+                in_=tokens[e][:].rearrange("p c t -> p (c t)"),
+            )
+
+        for t in range(2):
+            nc.vector.tensor_copy(rounded[t][:], planes[t][:])
+        for e in range(E):
+            for t in range(PACK):
+                pick(e, t)
+            if e == 0:
+                quantise_tokens(e)
+
+        a_banks, b_banks, relus, hidden, turned_banks, turned, hidden_codes, hidden_scales = {}, {}, {}, {}, {}, {}, {}, {}
+        y_banks, y_copies = {}, {}
+
+        def multiply_first(banks, name, words, scales, u):
+            e, g = u // PASSES, u % PASSES
+            banks[u] = psum_first.tile([P, HALF], F32, name=name)
+            nc.tensor.matmul_mx(
+                out=banks[u][:],
+                lhsT=token_codes[e][:].bitcast(FP8X4),
+                lhsT_scale=token_scales[e][:],
+                rhs=words[e][:, 2 * g * HALF : 2 * (g + 1) * HALF].bitcast(FP4X4),
+                rhs_scale=scales[:, e, g * HALF : (g + 1) * HALF],
+                start=True,
+                stop=True,
+            )
+
+        def multiply_a(u):
+            multiply_first(a_banks, "a", w1, s1, u)
+
+        def multiply_b(u):
+            multiply_first(b_banks, "b", w3, s3, u)
+
+        def bank_order(bank):
+            return bank[:].rearrange("s (m v d) -> s v m d", v=2, d=2)
+
+        def pair_order(tile):
+            return tile[:].rearrange("s (v m d) -> s v m d", v=2, d=2)
+
+        def rectify(u):
+            relus[u] = work.tile([P, HALF], F32, name="relu")
+            nc.scalar.activation(pair_order(relus[u]), bank_order(a_banks[u]), RELU)
+
+        def gate_hidden(u):
+            hidden[u] = work.tile([P, HALF], BF16, name="hidden")
+            nc.vector.tensor_tensor(pair_order(hidden[u]), bank_order(b_banks[u]), pair_order(relus[u]), MULT)
+
+        def turn(u):
+            pairs = hidden[u][:].bitcast(F32)
+            turned_banks[u] = psum_turned.tile([P, 2, C], F32, name="turned_bank")
+            for v in range(2):
+                nc.tensor.transpose(turned_banks[u][:, v, :], pairs[:, v * P : (v + 1) * P], identity[:])
+
+        def empty_turned(u):
+            turned[u] = work.tile([P, C, PACK], BF16, name="turned", align_bytes=64)
+            nc.scalar.copy(
+                turned[u][:].rearrange("p c t -> p (c t)").bitcast(F32).rearrange("p (c v) -> p c v", v=2),
+                turned_banks[u][:].rearrange("p v c -> p c v"),
+            )
+
+        def quantise_hidden(u):
+            hidden_codes[u] = work.tile([P, C], U32, name="hidden_codes", align_bytes=64)
+            hidden_scales[u] = work.tile([P, C], U8, name="hidden_scales", align_bytes=64)
+            nc.vector.quantize_mx(
+                out=hidden_codes[u][:].bitcast(FP8X4),
+                scales=hidden_scales[u][:],
+                in_=turned[u][:].rearrange("p c t -> p (c t)"),
+            )
+
+        def multiply_second(u):
+            e, g = u // PASSES, u % PASSES
+            if g == 0:
+                y_banks[e] = psum_second.tile([P, C], F32, name="y_bank")
+            nc.tensor.matmul_mx(
+                out=y_banks[e][:],
+                lhsT=w2[:, u, :].bitcast(FP4X4),
+                lhsT_scale=s2[:, u, :],
+                rhs=hidden_codes[u][:].bitcast(FP8X4),
+                rhs_scale=hidden_scales[u][:],
+                start=(g == 0),
+                stop=(g == PASSES - 1),
+            )
+
+        def take_out(e):
+            y_copies[e] = work.tile([P, C], F32, name="y_copy")
+            nc.scalar.copy(y_copies[e][:], y_banks[e][:])
+
+        def send_back(e):
+            nc.vector.tensor_tensor(
+                result[:].indirect(slots_of(places, e)), y_copies[e][:], gates[:, e * C : (e + 1) * C], MULT
+            )
+
+        calls = (
+            (multiply_a, 0, 0),
+            (multiply_a, 0, 1),
+            (rectify, 0, 0),
+            (quantise_hidden, 2, 0),
+            (multiply_b, 0, 0),
+            (quantise_hidden, 2, 1),
+            (take_out, 4, None),
+            (turn, 1, 0),
+            (turn, 1, 1),
+            (multiply_b, 0, 1),
+            (rectify, 0, 1),
+            (empty_turned, 1, 0),
+            (gate_hidden, 0, 0),
+            (quantise_tokens, -1, None),
+            (empty_turned, 1, 1),
+            (multiply_second, 3, 1),
+            (multiply_second, 2, 0),
+            (gate_hidden, 0, 1),
+            (send_back, 4, None),
+        )
+        longest_lag = max(lag for call, lag, g in calls)
+        for step in range(E + longest_lag):
+            for call, lag, g in calls:
+                e = step - lag
+                if 0 <= e < E and (call is not quantise_tokens or e > 0):
+                    call(e if g is None else e * PASSES + g)
+        nc.sync.dma_start(out, result[:])

@@ -23,6 +23,8 @@ PACK = 4
 HALF = 512
 PASSES = H // HALF
 SCALE_ROWS = 16
+GROUPS1 = ((0, 4),)
+GROUPS3 = ((0, 4),)
 LIST_COLS = C // 16
 
 
@@ -32,10 +34,11 @@ def tile_moe_two_glu_relu_kernel(
     nc = tc.nc
     with ExitStack() as ctx:
         keep = ctx.enter_context(tc.tile_pool(name="keep", bufs=1))
-        work = ctx.enter_context(tc.tile_pool(name="work", bufs=4))
-        psum_first = ctx.enter_context(tc.psum_pool(name="psum_first", bufs=2))
+        work = ctx.enter_context(tc.tile_pool(name="work", bufs=8))
+        psum_a = ctx.enter_context(tc.psum_pool(name="psum_a", bufs=2))
+        psum_b = ctx.enter_context(tc.psum_pool(name="psum_b", bufs=3))
         psum_turned = ctx.enter_context(tc.psum_pool(name="psum_turned", bufs=2))
-        psum_second = ctx.enter_context(tc.psum_pool(name="psum_second", bufs=2))
+        psum_second = ctx.enter_context(tc.psum_pool(name="psum_second", bufs=1))
 
         sources = keep.tile([P, E * LIST_COLS], U16, name="sources")
         places = keep.tile([P, E * LIST_COLS], U16, name="places")
@@ -44,8 +47,8 @@ def tile_moe_two_glu_relu_kernel(
         w1 = [keep.tile([P, 2 * H], U8, name="w1_%d" % e, align_bytes=64) for e in range(E)]
         w3 = [keep.tile([P, 2 * H], U8, name="w3_%d" % e, align_bytes=64) for e in range(E)]
         w2 = keep.tile([P, E * PASSES, 2 * N], U8, name="w2", align_bytes=64)
-        s1 = keep.tile([P, E, H], U8, name="s1", align_bytes=64)
-        s3 = keep.tile([P, E, H], U8, name="s3", align_bytes=64)
+        s1 = [keep.tile([P, b - a, H], U8, name="s1_%d" % a, align_bytes=64) for a, b in GROUPS1]
+        s3 = [keep.tile([P, b - a, H], U8, name="s3_%d" % a, align_bytes=64) for a, b in GROUPS3]
         s2 = keep.tile([P, E * PASSES, N], U8, name="s2", align_bytes=64)
         identity = keep.tile([P, P], F32, name="identity")
         result = keep.tile([P, T], F32, name="result")
@@ -53,7 +56,7 @@ def tile_moe_two_glu_relu_kernel(
         column = keep.tile([P, 1], F32, name="column")
         nc.gpsimd.memset(column[:], 0.0)
         nc.scalar.activation(column[:], column[:], RELU)
-        for scales in (s1, s3, s2):
+        for scales in s1[:1] + s3[:1] + [s2] + s1[1:] + s3[1:]:
             nc.vector.memset(scales[:].bitcast(I32), 0)
         make_identity(nc, identity[:])
         nc.gpsimd.memset(result[:], 0.0)
@@ -70,23 +73,23 @@ def tile_moe_two_glu_relu_kernel(
 
         load_plane(0)
         nc.sync.dma_start(sources[:], offs)
-        load_plane(1)
+        nc.sync.dma_start(places[:], dst)
         load_plane(2)
+        load_plane(1)
         load_plane(3)
-        load_scales(nc.sync, s1, w1_scales.bitcast(I32).rearrange("e s q i -> (e s) q i"))
+        load_scales(nc.sync, s1[0], w1_scales.bitcast(I32)[slice(*GROUPS1[0])].rearrange("e s q i -> (e s) q i"))
         load_words(w1, w1_words, 0)
-        load_scales(nc.sync, s3, w3_scales.bitcast(I32).rearrange("e s q i -> (e s) q i"))
+        load_scales(nc.sync, s3[0], w3_scales.bitcast(I32)[slice(*GROUPS3[0])].rearrange("e s q i -> (e s) q i"))
         load_words(w3, w3_words, 0)
         load_words(w1, w1_words, 1)
         load_words(w3, w3_words, 1)
         load_scales(nc.gpsimd, s2, w2_scales.bitcast(I32).rearrange("e s q n -> (e s) q n"))
-        nc.sync.dma_start(w2[:].bitcast(I32), w2_words.bitcast(I32).rearrange("e s p c -> p (e s) c"))
         load_words(w1, w1_words, 2)
         load_words(w3, w3_words, 2)
-        nc.sync.dma_start(places[:], dst)
+        nc.sync.dma_start(w2[:].bitcast(I32), w2_words.bitcast(I32).rearrange("e s p c -> p (e s) c"))
         load_words(w1, w1_words, 3)
-        load_words(w3, w3_words, 3)
         nc.sync.dma_start(gates[:], gate)
+        load_words(w3, w3_words, 3)
 
         rounded = [keep.tile([P, T], BF16, name="rounded%d" % t, align_bytes=64) for t in range(2)]
         tokens = [keep.tile([P, C, PACK], BF16, name="tokens%d" % e, align_bytes=64) for e in range(E)]
@@ -111,33 +114,39 @@ def tile_moe_two_glu_relu_kernel(
 
         for t in range(2):
             nc.vector.tensor_copy(rounded[t][:], planes[t][:])
-        for e in range(E):
-            for t in range(PACK):
+            for e in range(E):
                 pick(e, t)
-            if e == 0:
-                quantise_tokens(e)
+            if t == 0:
+                for e in range(E):
+                    pick(e, 2)
+        for e in range(E):
+            pick(e, 3)
+            if e > 0:
+                quantise_tokens(e - 1)
+        quantise_tokens(E - 1)
 
-        a_banks, b_banks, relus, hidden, turned_banks, turned, hidden_codes, hidden_scales = {}, {}, {}, {}, {}, {}, {}, {}
+        a_banks, b_banks, relus, hidden, turned_banks, turned, codes, scales = {}, {}, {}, {}, {}, {}, {}, {}
         y_banks, y_copies = {}, {}
 
-        def multiply_first(banks, name, words, scales, u):
+        def multiply_first(pool, banks, name, words, scale_tiles, groups, u):
             e, g = u // PASSES, u % PASSES
-            banks[u] = psum_first.tile([P, HALF], F32, name=name)
+            n = [a <= e < b for a, b in groups].index(True)
+            banks[u] = pool.tile([P, HALF], F32, name=name)
             nc.tensor.matmul_mx(
                 out=banks[u][:],
                 lhsT=token_codes[e][:].bitcast(FP8X4),
                 lhsT_scale=token_scales[e][:],
                 rhs=words[e][:, 2 * g * HALF : 2 * (g + 1) * HALF].bitcast(FP4X4),
-                rhs_scale=scales[:, e, g * HALF : (g + 1) * HALF],
+                rhs_scale=scale_tiles[n][:, e - groups[n][0], g * HALF : (g + 1) * HALF],
                 start=True,
                 stop=True,
             )
 
         def multiply_a(u):
-            multiply_first(a_banks, "a", w1, s1, u)
+            multiply_first(psum_a, a_banks, "a", w1, s1, GROUPS1, u)
 
         def multiply_b(u):
-            multiply_first(b_banks, "b", w3, s3, u)
+            multiply_first(psum_b, b_banks, "b", w3, s3, GROUPS3, u)
 
         def bank_order(bank):
             return bank[:].rearrange("s (m v d) -> s v m d", v=2, d=2)
@@ -153,41 +162,39 @@ def tile_moe_two_glu_relu_kernel(
             hidden[u] = work.tile([P, HALF], BF16, name="hidden")
             nc.vector.tensor_tensor(pair_order(hidden[u]), bank_order(b_banks[u]), pair_order(relus[u]), MULT)
 
-        def turn(u):
-            pairs = hidden[u][:].bitcast(F32)
-            turned_banks[u] = psum_turned.tile([P, 2, C], F32, name="turned_bank")
-            for v in range(2):
-                nc.tensor.transpose(turned_banks[u][:, v, :], pairs[:, v * P : (v + 1) * P], identity[:])
+        def turn(*us):
+            turned_banks[us] = psum_turned.tile([P, len(us), 2, C], F32, name="turned_bank")
+            for j, u in reversed(list(enumerate(us))):
+                pairs = hidden[u][:].bitcast(F32)
+                for v in range(2):
+                    nc.tensor.transpose(turned_banks[us][:, j, v, :], pairs[:, v * P : (v + 1) * P], identity[:])
 
-        def empty_turned(u):
-            turned[u] = work.tile([P, C, PACK], BF16, name="turned", align_bytes=64)
+        def empty_turned(*us):
+            turned[us] = work.tile([P, len(us) * C * PACK], BF16, name="turned", align_bytes=64)
             nc.scalar.copy(
-                turned[u][:].rearrange("p c t -> p (c t)").bitcast(F32).rearrange("p (c v) -> p c v", v=2),
-                turned_banks[u][:].rearrange("p v c -> p c v"),
+                turned[us][:].bitcast(F32).rearrange("p (j c v) -> p j c v", j=len(us), v=2),
+                turned_banks[us][:].rearrange("p j v c -> p j c v"),
             )
 
-        def quantise_hidden(u):
-            hidden_codes[u] = work.tile([P, C], U32, name="hidden_codes", align_bytes=64)
-            hidden_scales[u] = work.tile([P, C], U8, name="hidden_scales", align_bytes=64)
-            nc.vector.quantize_mx(
-                out=hidden_codes[u][:].bitcast(FP8X4),
-                scales=hidden_scales[u][:],
-                in_=turned[u][:].rearrange("p c t -> p (c t)"),
-            )
+        def quantise_hidden(*us):
+            codes[us] = work.tile([P, len(us) * C], U32, name="hidden_codes", align_bytes=64)
+            scales[us] = work.tile([P, len(us) * C], U8, name="hidden_scales", align_bytes=64)
+            nc.vector.quantize_mx(out=codes[us][:].bitcast(FP8X4), scales=scales[us][:], in_=turned[us][:])
 
-        def multiply_second(u):
-            e, g = u // PASSES, u % PASSES
-            if g == 0:
-                y_banks[e] = psum_second.tile([P, C], F32, name="y_bank")
-            nc.tensor.matmul_mx(
-                out=y_banks[e][:],
-                lhsT=w2[:, u, :].bitcast(FP4X4),
-                lhsT_scale=s2[:, u, :],
-                rhs=hidden_codes[u][:].bitcast(FP8X4),
-                rhs_scale=hidden_scales[u][:],
-                start=(g == 0),
-                stop=(g == PASSES - 1),
-            )
+        def multiply_second(*us):
+            for j, u in enumerate(us):
+                e, g = u // PASSES, u % PASSES
+                if g == 0:
+                    y_banks[e] = psum_second.tile([P, C], F32, name="y_bank")
+                nc.tensor.matmul_mx(
+                    out=y_banks[e][:],
+                    lhsT=w2[:, u, :].bitcast(FP4X4),
+                    lhsT_scale=s2[:, u, :],
+                    rhs=codes[us][:, j * C : (j + 1) * C].bitcast(FP8X4),
+                    rhs_scale=scales[us][:, j * C : (j + 1) * C],
+                    start=(g == 0),
+                    stop=(g == PASSES - 1),
+                )
 
         def take_out(e):
             y_copies[e] = work.tile([P, C], F32, name="y_copy")
@@ -198,31 +205,64 @@ def tile_moe_two_glu_relu_kernel(
                 result[:].indirect(slots_of(places, e)), y_copies[e][:], gates[:, e * C : (e + 1) * C], MULT
             )
 
-        calls = (
-            (multiply_a, 0, 0),
-            (multiply_a, 0, 1),
-            (rectify, 0, 0),
-            (quantise_hidden, 2, 0),
-            (multiply_b, 0, 0),
-            (quantise_hidden, 2, 1),
-            (take_out, 4, None),
-            (turn, 1, 0),
-            (turn, 1, 1),
-            (multiply_b, 0, 1),
-            (rectify, 0, 1),
-            (empty_turned, 1, 0),
-            (gate_hidden, 0, 0),
-            (quantise_tokens, -1, None),
-            (empty_turned, 1, 1),
-            (multiply_second, 3, 1),
-            (multiply_second, 2, 0),
-            (gate_hidden, 0, 1),
-            (send_back, 4, None),
-        )
-        longest_lag = max(lag for call, lag, g in calls)
-        for step in range(E + longest_lag):
-            for call, lag, g in calls:
-                e = step - lag
-                if 0 <= e < E and (call is not quantise_tokens or e > 0):
-                    call(e if g is None else e * PASSES + g)
+        multiply_a(0)
+        multiply_a(1)
+        rectify(0)
+        rectify(1)
+        multiply_b(0)
+        multiply_b(1)
+        multiply_a(2)
+        gate_hidden(0)
+        multiply_a(3)
+        multiply_b(2)
+        rectify(2)
+        gate_hidden(1)
+        multiply_b(3)
+        rectify(3)
+        gate_hidden(2)
+        multiply_a(4)
+        turn(0, 1)
+        multiply_b(4)
+        rectify(4)
+        gate_hidden(3)
+        multiply_a(5)
+        multiply_b(5)
+        empty_turned(0, 1)
+        gate_hidden(4)
+        rectify(5)
+        turn(2, 3)
+        quantise_hidden(0, 1)
+        multiply_a(6)
+        multiply_second(0, 1)
+        gate_hidden(5)
+        empty_turned(2, 3)
+        multiply_a(7)
+        take_out(0)
+        multiply_b(6)
+        rectify(6)
+        quantise_hidden(2, 3)
+        turn(4, 5)
+        send_back(0)
+        multiply_b(7)
+        rectify(7)
+        multiply_second(2, 3)
+        gate_hidden(6)
+        empty_turned(4, 5)
+        gate_hidden(7)
+        turn(6)
+        take_out(1)
+        quantise_hidden(4, 5)
+        turn(7)
+        empty_turned(6)
+        send_back(1)
+        multiply_second(4, 5)
+        empty_turned(7)
+        take_out(2)
+        quantise_hidden(6)
+        quantise_hidden(7)
+        multiply_second(6)
+        multiply_second(7)
+        send_back(2)
+        take_out(3)
+        send_back(3)
         nc.sync.dma_start(out, result[:])

@@ -23,9 +23,13 @@ PACK = 4
 HALF = 512
 PASSES = H // HALF
 SCALE_ROWS = 16
-GROUPS1 = ((0, 4),)
-GROUPS3 = ((0, 4),)
 LIST_COLS = C // 16
+EARLY = 2
+
+A_BANKS = ((0, 1), (5, 6), (0, 1), (0, 1))
+B_BANKS = ((2, 3), (4, 7), (2, 3), (4, 7))
+TURNED_BANKS = (5, 6, 5, 6)
+Y_BANKS = (2, 3, 0, 1)
 
 
 def tile_moe_two_glu_relu_kernel(
@@ -34,21 +38,25 @@ def tile_moe_two_glu_relu_kernel(
     nc = tc.nc
     with ExitStack() as ctx:
         keep = ctx.enter_context(tc.tile_pool(name="keep", bufs=1))
-        work = ctx.enter_context(tc.tile_pool(name="work", bufs=8))
-        psum_a = ctx.enter_context(tc.psum_pool(name="psum_a", bufs=2))
-        psum_b = ctx.enter_context(tc.psum_pool(name="psum_b", bufs=3))
-        psum_turned = ctx.enter_context(tc.psum_pool(name="psum_turned", bufs=2))
-        psum_second = ctx.enter_context(tc.psum_pool(name="psum_second", bufs=1))
+        psum = ctx.enter_context(tc.psum_pool(name="psum", bufs=1))
+        banks = [psum.tile([P, HALF], F32, name="bank%d" % n) for n in range(8)]
+
+        def per_expert(name, shape, dtype):
+            return [keep.tile(shape, dtype, name="%s%d" % (name, e), align_bytes=64) for e in range(E)]
+
+        def per_half(name, dtype):
+            return [[keep.tile([P, HALF], dtype, name="%s%d_%d" % (name, e, g)) for g in range(PASSES)] for e in range(E)]
 
         sources = keep.tile([P, E * LIST_COLS], U16, name="sources")
         places = keep.tile([P, E * LIST_COLS], U16, name="places")
         planes = [keep.tile([P, T], F32, name="plane%d" % t) for t in range(PACK)]
         gates = keep.tile([P, E * C], F32, name="gates")
-        w1 = [keep.tile([P, 2 * H], U8, name="w1_%d" % e, align_bytes=64) for e in range(E)]
-        w3 = [keep.tile([P, 2 * H], U8, name="w3_%d" % e, align_bytes=64) for e in range(E)]
+        w1 = per_expert("w1_", [P, 2 * H], U8)
+        w3 = per_expert("w3_", [P, 2 * H], U8)
         w2 = keep.tile([P, E * PASSES, 2 * N], U8, name="w2", align_bytes=64)
-        s1 = [keep.tile([P, b - a, H], U8, name="s1_%d" % a, align_bytes=64) for a, b in GROUPS1]
-        s3 = [keep.tile([P, b - a, H], U8, name="s3_%d" % a, align_bytes=64) for a, b in GROUPS3]
+        s1 = keep.tile([P, E, H], U8, name="s1", align_bytes=64)
+        s3_early = keep.tile([P, EARLY, H], U8, name="s3_early", align_bytes=64)
+        s3_late = w1[0][:].rearrange("p (e i) -> p e i", i=H)
         s2 = keep.tile([P, E * PASSES, N], U8, name="s2", align_bytes=64)
         identity = keep.tile([P, P], F32, name="identity")
         result = keep.tile([P, T], F32, name="result")
@@ -56,7 +64,7 @@ def tile_moe_two_glu_relu_kernel(
         column = keep.tile([P, 1], F32, name="column")
         nc.gpsimd.memset(column[:], 0.0)
         nc.scalar.activation(column[:], column[:], RELU)
-        for scales in s1[:1] + s3[:1] + [s2] + s1[1:] + s3[1:]:
+        for scales in (s1, s3_early, s2):
             nc.vector.memset(scales[:].bitcast(I32), 0)
         make_identity(nc, identity[:])
         nc.gpsimd.memset(result[:], 0.0)
@@ -67,9 +75,10 @@ def tile_moe_two_glu_relu_kernel(
         def load_words(tiles, words, e):
             nc.sync.dma_start(tiles[e][:].bitcast(I32), words[e, 0].bitcast(I32))
 
-        def load_scales(queue, tile, rows):
+        def load_scales(queue, into, rows):
+            rows = rows.bitcast(I32).rearrange("e s q c -> q (e s) c")
             for r in range(4):
-                queue.dma_start(tile[:].bitcast(I32)[r:P:32, :, :], rows[:, r:SCALE_ROWS:4, :].rearrange("m q c -> q m c"))
+                queue.dma_start(into.bitcast(I32)[r:P:32, :, :], rows[r:SCALE_ROWS:4, :, :])
 
         load_plane(0)
         nc.sync.dma_start(sources[:], offs)
@@ -77,33 +86,26 @@ def tile_moe_two_glu_relu_kernel(
         load_plane(2)
         load_plane(1)
         load_plane(3)
-        load_scales(nc.sync, s1[0], w1_scales.bitcast(I32)[slice(*GROUPS1[0])].rearrange("e s q i -> (e s) q i"))
+        load_scales(nc.sync, s1[:], w1_scales)
         load_words(w1, w1_words, 0)
-        load_scales(nc.sync, s3[0], w3_scales.bitcast(I32)[slice(*GROUPS3[0])].rearrange("e s q i -> (e s) q i"))
-        load_words(w3, w3_words, 0)
         load_words(w1, w1_words, 1)
+        load_scales(nc.sync, s3_early[:], w3_scales[:EARLY])
+        load_words(w3, w3_words, 0)
         load_words(w3, w3_words, 1)
-        load_scales(nc.gpsimd, s2, w2_scales.bitcast(I32).rearrange("e s q n -> (e s) q n"))
-        load_words(w1, w1_words, 2)
-        load_words(w3, w3_words, 2)
+        load_scales(nc.gpsimd, s2[:], w2_scales)
+        for e in range(EARLY, E):
+            load_words(w1, w1_words, e)
+            load_words(w3, w3_words, e)
         nc.sync.dma_start(w2[:].bitcast(I32), w2_words.bitcast(I32).rearrange("e s p c -> p (e s) c"))
-        load_words(w1, w1_words, 3)
         nc.sync.dma_start(gates[:], gate)
-        load_words(w3, w3_words, 3)
 
         rounded = [keep.tile([P, T], BF16, name="rounded%d" % t, align_bytes=64) for t in range(2)]
-        tokens = [keep.tile([P, C, PACK], BF16, name="tokens%d" % e, align_bytes=64) for e in range(E)]
-        token_codes = [keep.tile([P, C], U32, name="token_codes%d" % e, align_bytes=64) for e in range(E)]
-        token_scales = [keep.tile([P, C], U8, name="token_scales%d" % e, align_bytes=64) for e in range(E)]
+        tokens = per_expert("tokens", [P, C, PACK], BF16)
+        token_codes = per_expert("token_codes", [P, C], U32)
+        token_scales = per_expert("token_scales", [P, C], U8)
 
         def slots_of(offsets, e):
             return offsets[:, e * LIST_COLS : (e + 1) * LIST_COLS]
-
-        def pick(e, t):
-            if t < 2:
-                nc.scalar.activation(tokens[e][:, :, t], rounded[t][:].indirect(slots_of(sources, e)), COPY)
-            else:
-                nc.vector.tensor_copy(tokens[e][:, :, t], planes[t][:].indirect(slots_of(sources, e)))
 
         def quantise_tokens(e):
             nc.vector.quantize_mx(
@@ -115,38 +117,37 @@ def tile_moe_two_glu_relu_kernel(
         for t in range(2):
             nc.vector.tensor_copy(rounded[t][:], planes[t][:])
             for e in range(E):
-                pick(e, t)
-            if t == 0:
-                for e in range(E):
-                    pick(e, 2)
-        for e in range(E):
-            pick(e, 3)
-            if e > 0:
-                quantise_tokens(e - 1)
+                nc.scalar.activation(tokens[e][:, :, t], rounded[t][:].indirect(slots_of(sources, e)), COPY)
+            for e in range(E):
+                nc.vector.tensor_copy(tokens[e][:, :, t + 2], planes[t + 2][:].indirect(slots_of(sources, e)))
+                if t == 1 and e > 0:
+                    quantise_tokens(e - 1)
         quantise_tokens(E - 1)
 
-        a_banks, b_banks, relus, hidden, turned_banks, turned, codes, scales = {}, {}, {}, {}, {}, {}, {}, {}
-        y_banks, y_copies = {}, {}
+        relus = per_half("relu", F32)
+        hidden = per_half("hidden", BF16)
+        turned = per_expert("turned", [P, PASSES * C * PACK], BF16)
+        hidden_codes = per_expert("hidden_codes", [P, PASSES * C], U32)
+        hidden_scales = per_expert("hidden_scales", [P, PASSES * C], U8)
+        y_copies = per_expert("y_copy", [P, C], F32)
 
-        def multiply_first(pool, banks, name, words, scale_tiles, groups, u):
-            e, g = u // PASSES, u % PASSES
-            n = [a <= e < b for a, b in groups].index(True)
-            banks[u] = pool.tile([P, HALF], F32, name=name)
-            nc.tensor.matmul_mx(
-                out=banks[u][:],
-                lhsT=token_codes[e][:].bitcast(FP8X4),
-                lhsT_scale=token_scales[e][:],
-                rhs=words[e][:, 2 * g * HALF : 2 * (g + 1) * HALF].bitcast(FP4X4),
-                rhs_scale=scale_tiles[n][:, e - groups[n][0], g * HALF : (g + 1) * HALF],
-                start=True,
-                stop=True,
-            )
+        def multiply_first(e, bank_numbers, words, scales):
+            for g in range(PASSES):
+                nc.tensor.matmul_mx(
+                    out=banks[bank_numbers[g]][:],
+                    lhsT=token_codes[e][:].bitcast(FP8X4),
+                    lhsT_scale=token_scales[e][:],
+                    rhs=words[:, 2 * g * HALF : 2 * (g + 1) * HALF].bitcast(FP4X4),
+                    rhs_scale=scales[:, g * HALF : (g + 1) * HALF],
+                    start=True,
+                    stop=True,
+                )
 
-        def multiply_a(u):
-            multiply_first(psum_a, a_banks, "a", w1, s1, GROUPS1, u)
+        def multiply_a(e):
+            multiply_first(e, A_BANKS[e], w1[e], s1[:, e, :])
 
-        def multiply_b(u):
-            multiply_first(psum_b, b_banks, "b", w3, s3, GROUPS3, u)
+        def multiply_b(e):
+            multiply_first(e, B_BANKS[e], w3[e], s3_early[:, e, :] if e < EARLY else s3_late[:, e - EARLY, :])
 
         def bank_order(bank):
             return bank[:].rearrange("s (m v d) -> s v m d", v=2, d=2)
@@ -154,115 +155,70 @@ def tile_moe_two_glu_relu_kernel(
         def pair_order(tile):
             return tile[:].rearrange("s (v m d) -> s v m d", v=2, d=2)
 
-        def rectify(u):
-            relus[u] = work.tile([P, HALF], F32, name="relu")
-            nc.scalar.activation(pair_order(relus[u]), bank_order(a_banks[u]), RELU)
+        def rectify(e):
+            for g in range(PASSES):
+                nc.scalar.activation(pair_order(relus[e][g]), bank_order(banks[A_BANKS[e][g]]), RELU)
+            if e == 0:
+                load_scales(nc.scalar, s3_late, w3_scales[EARLY:])
 
-        def gate_hidden(u):
-            hidden[u] = work.tile([P, HALF], BF16, name="hidden")
-            nc.vector.tensor_tensor(pair_order(hidden[u]), bank_order(b_banks[u]), pair_order(relus[u]), MULT)
+        def gate_hidden(e):
+            for g in range(PASSES):
+                nc.vector.tensor_tensor(
+                    pair_order(hidden[e][g]), bank_order(banks[B_BANKS[e][g]]), pair_order(relus[e][g]), MULT
+                )
 
-        def turn(*us):
-            turned_banks[us] = psum_turned.tile([P, len(us), 2, C], F32, name="turned_bank")
-            for j, u in reversed(list(enumerate(us))):
-                pairs = hidden[u][:].bitcast(F32)
+        def turned_bank(e):
+            return banks[TURNED_BANKS[e]][:].rearrange("p (g v c) -> p g v c", g=PASSES, v=2)
+
+        def turn(e):
+            for g in reversed(range(PASSES)):
+                pairs = hidden[e][g][:].bitcast(F32)
                 for v in range(2):
-                    nc.tensor.transpose(turned_banks[us][:, j, v, :], pairs[:, v * P : (v + 1) * P], identity[:])
+                    nc.tensor.transpose(turned_bank(e)[:, g, v, :], pairs[:, v * P : (v + 1) * P], identity[:])
 
-        def empty_turned(*us):
-            turned[us] = work.tile([P, len(us) * C * PACK], BF16, name="turned", align_bytes=64)
+        def empty_turned(e):
             nc.scalar.copy(
-                turned[us][:].bitcast(F32).rearrange("p (j c v) -> p j c v", j=len(us), v=2),
-                turned_banks[us][:].rearrange("p j v c -> p j c v"),
+                turned[e][:].bitcast(F32).rearrange("p (g c v) -> p g c v", g=PASSES, v=2),
+                turned_bank(e).rearrange("p g v c -> p g c v"),
             )
 
-        def quantise_hidden(*us):
-            codes[us] = work.tile([P, len(us) * C], U32, name="hidden_codes", align_bytes=64)
-            scales[us] = work.tile([P, len(us) * C], U8, name="hidden_scales", align_bytes=64)
-            nc.vector.quantize_mx(out=codes[us][:].bitcast(FP8X4), scales=scales[us][:], in_=turned[us][:])
+        def quantise_hidden(e):
+            nc.vector.quantize_mx(out=hidden_codes[e][:].bitcast(FP8X4), scales=hidden_scales[e][:], in_=turned[e][:])
 
-        def multiply_second(*us):
-            for j, u in enumerate(us):
-                e, g = u // PASSES, u % PASSES
-                if g == 0:
-                    y_banks[e] = psum_second.tile([P, C], F32, name="y_bank")
+        def multiply_second(e):
+            for g in range(PASSES):
                 nc.tensor.matmul_mx(
-                    out=y_banks[e][:],
-                    lhsT=w2[:, u, :].bitcast(FP4X4),
-                    lhsT_scale=s2[:, u, :],
-                    rhs=codes[us][:, j * C : (j + 1) * C].bitcast(FP8X4),
-                    rhs_scale=scales[us][:, j * C : (j + 1) * C],
+                    out=banks[Y_BANKS[e]][:, :C],
+                    lhsT=w2[:, e * PASSES + g, :].bitcast(FP4X4),
+                    lhsT_scale=s2[:, e * PASSES + g, :],
+                    rhs=hidden_codes[e][:, g * C : (g + 1) * C].bitcast(FP8X4),
+                    rhs_scale=hidden_scales[e][:, g * C : (g + 1) * C],
                     start=(g == 0),
                     stop=(g == PASSES - 1),
                 )
 
         def take_out(e):
-            y_copies[e] = work.tile([P, C], F32, name="y_copy")
-            nc.scalar.copy(y_copies[e][:], y_banks[e][:])
+            nc.scalar.copy(y_copies[e][:], banks[Y_BANKS[e]][:, :C])
 
         def send_back(e):
             nc.vector.tensor_tensor(
                 result[:].indirect(slots_of(places, e)), y_copies[e][:], gates[:, e * C : (e + 1) * C], MULT
             )
 
-        multiply_a(0)
-        multiply_a(1)
-        rectify(0)
-        rectify(1)
-        multiply_b(0)
-        multiply_b(1)
-        multiply_a(2)
-        gate_hidden(0)
-        multiply_a(3)
-        multiply_b(2)
-        rectify(2)
-        gate_hidden(1)
-        multiply_b(3)
-        rectify(3)
-        gate_hidden(2)
-        multiply_a(4)
-        turn(0, 1)
-        multiply_b(4)
-        rectify(4)
-        gate_hidden(3)
-        multiply_a(5)
-        multiply_b(5)
-        empty_turned(0, 1)
-        gate_hidden(4)
-        rectify(5)
-        turn(2, 3)
-        quantise_hidden(0, 1)
-        multiply_a(6)
-        multiply_second(0, 1)
-        gate_hidden(5)
-        empty_turned(2, 3)
-        multiply_a(7)
-        take_out(0)
-        multiply_b(6)
-        rectify(6)
-        quantise_hidden(2, 3)
-        turn(4, 5)
-        send_back(0)
-        multiply_b(7)
-        rectify(7)
-        multiply_second(2, 3)
-        gate_hidden(6)
-        empty_turned(4, 5)
-        gate_hidden(7)
-        turn(6)
-        take_out(1)
-        quantise_hidden(4, 5)
-        turn(7)
-        empty_turned(6)
-        send_back(1)
-        multiply_second(4, 5)
-        empty_turned(7)
-        take_out(2)
-        quantise_hidden(6)
-        quantise_hidden(7)
-        multiply_second(6)
-        multiply_second(7)
-        send_back(2)
-        take_out(3)
-        send_back(3)
+        calls = (
+            (multiply_a, 0),
+            (multiply_b, 0),
+            (rectify, 0),
+            (gate_hidden, 1),
+            (quantise_hidden, 3),
+            (turn, 2),
+            (empty_turned, 2),
+            (multiply_second, 3),
+            (send_back, 4),
+            (take_out, 3),
+        )
+        for step in range(E + max(lag for call, lag in calls)):
+            for call, lag in calls:
+                if 0 <= step - lag < E:
+                    call(step - lag)
         nc.sync.dma_start(out, result[:])

@@ -82,7 +82,6 @@ def tile_moe_two_glu_relu_kernel(
 
         load_plane(0)
         nc.sync.dma_start(sources[:], offs)
-        nc.sync.dma_start(places[:], dst)
         load_plane(2)
         load_plane(1)
         load_plane(3)
@@ -97,6 +96,7 @@ def tile_moe_two_glu_relu_kernel(
             load_words(w1, w1_words, e)
             load_words(w3, w3_words, e)
         nc.sync.dma_start(w2[:].bitcast(I32), w2_words.bitcast(I32).rearrange("e s p c -> p (e s) c"))
+        nc.sync.dma_start(places[:], dst)
         nc.sync.dma_start(gates[:], gate)
 
         rounded = [keep.tile([P, T], BF16, name="rounded%d" % t, align_bytes=64) for t in range(2)]

@@ -24,12 +24,14 @@ HALF = 512
 PASSES = H // HALF
 SCALE_ROWS = 16
 LIST_COLS = C // 16
-EARLY = 2
+W2_FIRST = 2
+PAIR = 2
 
-A_BANKS = ((0, 1), (5, 6), (0, 1), (0, 1))
-B_BANKS = ((2, 3), (4, 7), (2, 3), (4, 7))
-TURNED_BANKS = (5, 6, 5, 6)
-Y_BANKS = (2, 3, 0, 1)
+A_BANKS = ((0, 1), (4, 5), (0, 1), (0, 1))
+B_BANKS = ((2, 3), (6, 7), (2, 3), (6, 7))
+TURNED_BANKS = ((4, 4), (5, 5), (0, 0), (1, 1))
+Y_BANKS = (2, 3, 4, 5)
+GATE_BANK = 7
 
 
 def tile_moe_two_glu_relu_kernel(
@@ -44,30 +46,40 @@ def tile_moe_two_glu_relu_kernel(
         def per_expert(name, shape, dtype):
             return [keep.tile(shape, dtype, name="%s%d" % (name, e), align_bytes=64) for e in range(E)]
 
+        def per_pair(name, shape):
+            return [keep.tile(shape, U8, name="%s%d" % (name, q), align_bytes=64) for q in range(E // PAIR)]
+
         def per_half(name, dtype):
-            return [[keep.tile([P, HALF], dtype, name="%s%d_%d" % (name, e, g)) for g in range(PASSES)] for e in range(E)]
+            return [[keep.tile([P, HALF], dtype, name="%s%d_%d" % (name, e, g), tag="%s%d_%d" % (name, e, g), align_bytes=64) for g in range(PASSES)] for e in range(E)]
 
         sources = keep.tile([P, E * LIST_COLS], U16, name="sources")
         places = keep.tile([P, E * LIST_COLS], U16, name="places")
-        planes = [keep.tile([P, T], F32, name="plane%d" % t) for t in range(PACK)]
+        planes = [keep.tile([P, T], F32, name="plane%d" % t, tag="plane%d" % t) for t in range(PACK)]
+        gate_row = keep.tile([P, PACK], F32, name="gate_row")
         gates = keep.tile([P, E * C], F32, name="gates")
         w1 = per_expert("w1_", [P, 2 * H], U8)
         w3 = per_expert("w3_", [P, 2 * H], U8)
-        w2 = keep.tile([P, E * PASSES, 2 * N], U8, name="w2", align_bytes=64)
-        s1 = keep.tile([P, E, H], U8, name="s1", align_bytes=64)
-        s3_early = keep.tile([P, EARLY, H], U8, name="s3_early", align_bytes=64)
-        s3_late = w1[0][:].rearrange("p (e i) -> p e i", i=H)
+        w2_first = keep.tile([P, W2_FIRST * PASSES, 2 * N], U8, name="w2_first", align_bytes=64)
+        w2_rest = keep.tile([P, (E - W2_FIRST) * PASSES, 2 * N], U8, name="w2_rest", align_bytes=64)
+        s1_all = keep.tile([P, E, H], U8, name="s1", align_bytes=64)
+        s1 = [s1_all[:, :PAIR, :], s1_all[:, PAIR:, :]]
+        s3 = per_pair("s3_", [P, PAIR, H])
         s2 = keep.tile([P, E * PASSES, N], U8, name="s2", align_bytes=64)
         identity = keep.tile([P, P], F32, name="identity")
-        result = keep.tile([P, T], F32, name="result")
 
         column = keep.tile([P, 1], F32, name="column")
         nc.gpsimd.memset(column[:], 0.0)
         nc.scalar.activation(column[:], column[:], RELU)
-        for scales in (s1, s3_early, s2):
+        for scales in (s1_all, s3[0], s2, s3[1]):
             nc.vector.memset(scales[:].bitcast(I32), 0)
+        idle_codes = keep.tile([P, HALF], U32, name="idle_codes", align_bytes=64)
+        idle_scales = keep.tile([P, HALF], U8, name="idle_scales", align_bytes=64)
+        nc.vector.quantize_mx(
+            out=idle_codes[:].bitcast(FP8X4),
+            scales=idle_scales[:],
+            in_=s1_all[:].rearrange("p e i -> p (e i)").bitcast(BF16),
+        )
         make_identity(nc, identity[:])
-        nc.gpsimd.memset(result[:], 0.0)
 
         def load_plane(t):
             nc.sync.dma_start(planes[t][:], xT.rearrange("(p t) n -> p t n", t=PACK)[:, t, :])
@@ -80,24 +92,49 @@ def tile_moe_two_glu_relu_kernel(
             for r in range(4):
                 queue.dma_start(into.bitcast(I32)[r:P:32, :, :], rows[r:SCALE_ROWS:4, :, :])
 
+        def pair_of(tensor, q):
+            return tensor[q * PAIR : (q + 1) * PAIR]
+
+        def load_second_words(tile, words):
+            nc.sync.dma_start(tile[:].bitcast(I32), words.bitcast(I32).rearrange("e s p c -> p (e s) c"))
+
         load_plane(0)
         nc.sync.dma_start(sources[:], offs)
+        nc.sync.dma_start(gate_row[:], gate[0].rearrange("(p u) -> p u", u=PACK))
         load_plane(2)
         load_plane(1)
         load_plane(3)
-        load_scales(nc.sync, s1[:], w1_scales)
         load_words(w1, w1_words, 0)
-        load_words(w1, w1_words, 1)
-        load_scales(nc.sync, s3_early[:], w3_scales[:EARLY])
         load_words(w3, w3_words, 0)
-        load_words(w3, w3_words, 1)
+        load_scales(nc.sync,s1_all[:],w1_scales)
+        load_scales(nc.sync, s3[0][:], pair_of(w3_scales, 0))
         load_scales(nc.gpsimd, s2[:], w2_scales)
-        for e in range(EARLY, E):
-            load_words(w1, w1_words, e)
-            load_words(w3, w3_words, e)
-        nc.sync.dma_start(w2[:].bitcast(I32), w2_words.bitcast(I32).rearrange("e s p c -> p (e s) c"))
+        load_words(w1, w1_words, 1)
+        load_words(w3, w3_words, 1)
+        load_words(w1, w1_words, 2)
+        load_scales(nc.sync, s3[1][:], pair_of(w3_scales, 1))
+        load_words(w3, w3_words, 2)
+        load_words(w1, w1_words, 3)
+        load_words(w3, w3_words, 3)
+        load_second_words(w2_first, w2_words[:W2_FIRST])
         nc.sync.dma_start(places[:], dst)
-        nc.sync.dma_start(gates[:], gate)
+        load_second_words(w2_rest, w2_words[W2_FIRST:])
+
+        spread = banks[GATE_BANK][:].rearrange("n (u p) -> n u p", u=PACK)
+        for u in range(PACK):
+            nc.tensor.transpose(spread[:, u, :], gate_row[:, u : u + 1].to_broadcast([P, P]), identity[:])
+        nc.scalar.copy(gates[:].rearrange("n (p u) -> n p u", u=PACK), spread.rearrange("n u p -> n p u"))
+
+        for repeat in range(3):
+            nc.tensor.matmul_mx(
+                out=banks[6][:],
+                lhsT=w1[0][:, : 2 * P].bitcast(FP4X4),
+                lhsT_scale=idle_scales[:, :P],
+                rhs=idle_codes[:].bitcast(FP8X4),
+                rhs_scale=idle_scales[:],
+                start=True,
+                stop=True,
+            )
 
         rounded = [keep.tile([P, T], BF16, name="rounded%d" % t, align_bytes=64) for t in range(2)]
         tokens = per_expert("tokens", [P, C, PACK], BF16)
@@ -123,31 +160,37 @@ def tile_moe_two_glu_relu_kernel(
                 if t == 1 and e > 0:
                     quantise_tokens(e - 1)
         quantise_tokens(E - 1)
+        result = keep.tile([P, T], F32, name="result", tag="plane3")
+        nc.vector.memset(result[:], 0.0)
 
         relus = per_half("relu", F32)
         hidden = per_half("hidden", BF16)
         turned = per_expert("turned", [P, PASSES * C * PACK], BF16)
-        hidden_codes = per_expert("hidden_codes", [P, PASSES * C], U32)
+        hidden_codes = [
+            keep.tile([P, PASSES * C], U32, name="hidden_codes%d" % e, align_bytes=64, tag="relu2_0" if e == 1 else "hidden_codes%d" % e)
+            for e in range(E)
+        ]
         hidden_scales = per_expert("hidden_scales", [P, PASSES * C], U8)
         y_copies = per_expert("y_copy", [P, C], F32)
 
-        def multiply_first(e, bank_numbers, words, scales):
-            for g in range(PASSES):
-                nc.tensor.matmul_mx(
-                    out=banks[bank_numbers[g]][:],
-                    lhsT=token_codes[e][:].bitcast(FP8X4),
-                    lhsT_scale=token_scales[e][:],
-                    rhs=words[:, 2 * g * HALF : 2 * (g + 1) * HALF].bitcast(FP4X4),
-                    rhs_scale=scales[:, g * HALF : (g + 1) * HALF],
-                    start=True,
-                    stop=True,
-                )
+        def multiply_first(e, g, bank, words, scales):
+            nc.tensor.matmul_mx(
+                out=bank[:],
+                lhsT=token_codes[e][:].bitcast(FP8X4),
+                lhsT_scale=token_scales[e][:],
+                rhs=words[e][:, 2 * g * HALF : 2 * (g + 1) * HALF].bitcast(FP4X4),
+                rhs_scale=scales[e // PAIR][:, e % PAIR, g * HALF : (g + 1) * HALF],
+                start=True,
+                stop=True,
+            )
 
         def multiply_a(e):
-            multiply_first(e, A_BANKS[e], w1[e], s1[:, e, :])
+            for g in range(PASSES):
+                multiply_first(e, g, banks[A_BANKS[e][g]], w1, s1)
 
         def multiply_b(e):
-            multiply_first(e, B_BANKS[e], w3[e], s3_early[:, e, :] if e < EARLY else s3_late[:, e - EARLY, :])
+            for g in range(PASSES):
+                multiply_first(e, g, banks[B_BANKS[e][g]], w3, s3)
 
         def bank_order(bank):
             return bank[:].rearrange("s (m v d) -> s v m d", v=2, d=2)
@@ -158,8 +201,6 @@ def tile_moe_two_glu_relu_kernel(
         def rectify(e):
             for g in range(PASSES):
                 nc.scalar.activation(pair_order(relus[e][g]), bank_order(banks[A_BANKS[e][g]]), RELU)
-            if e == 0:
-                load_scales(nc.scalar, s3_late, w3_scales[EARLY:])
 
         def gate_hidden(e):
             for g in range(PASSES):
@@ -167,29 +208,33 @@ def tile_moe_two_glu_relu_kernel(
                     pair_order(hidden[e][g]), bank_order(banks[B_BANKS[e][g]]), pair_order(relus[e][g]), MULT
                 )
 
-        def turned_bank(e):
-            return banks[TURNED_BANKS[e]][:].rearrange("p (g v c) -> p g v c", g=PASSES, v=2)
+        def turned_bank(e, g):
+            return banks[TURNED_BANKS[e][g]][:].rearrange("p (g v c) -> p g v c", g=PASSES, v=2)
 
-        def turn(e):
-            for g in reversed(range(PASSES)):
+        def turn(e, first=0, last=PASSES):
+            for g in reversed(range(first, last)):
                 pairs = hidden[e][g][:].bitcast(F32)
                 for v in range(2):
-                    nc.tensor.transpose(turned_bank(e)[:, g, v, :], pairs[:, v * P : (v + 1) * P], identity[:])
+                    nc.tensor.transpose(turned_bank(e, g)[:, g, v, :], pairs[:, v * P : (v + 1) * P], identity[:])
 
-        def empty_turned(e):
+        def empty_turned(e, first=0, last=PASSES):
             nc.scalar.copy(
-                turned[e][:].bitcast(F32).rearrange("p (g c v) -> p g c v", g=PASSES, v=2),
-                turned_bank(e).rearrange("p g v c -> p g c v"),
+                turned[e][:].bitcast(F32).rearrange("p (g c v) -> p g c v", g=PASSES, v=2)[:, first:last],
+                turned_bank(e, first).rearrange("p g v c -> p g c v")[:, first:last],
             )
 
-        def quantise_hidden(e):
-            nc.vector.quantize_mx(out=hidden_codes[e][:].bitcast(FP8X4), scales=hidden_scales[e][:], in_=turned[e][:])
+        def quantise_hidden(e, first=0, last=PASSES):
+            nc.vector.quantize_mx(
+                out=hidden_codes[e][:, first * C : last * C].bitcast(FP8X4),
+                scales=hidden_scales[e][:, first * C : last * C],
+                in_=turned[e][:, first * C * PACK : last * C * PACK],
+            )
 
         def multiply_second(e):
             for g in range(PASSES):
                 nc.tensor.matmul_mx(
                     out=banks[Y_BANKS[e]][:, :C],
-                    lhsT=w2[:, e * PASSES + g, :].bitcast(FP4X4),
+                    lhsT=(w2_first[:, e * PASSES + g, :] if e < W2_FIRST else w2_rest[:, (e - W2_FIRST) * PASSES + g, :]).bitcast(FP4X4),
                     lhsT_scale=s2[:, e * PASSES + g, :],
                     rhs=hidden_codes[e][:, g * C : (g + 1) * C].bitcast(FP8X4),
                     rhs_scale=hidden_scales[e][:, g * C : (g + 1) * C],
@@ -205,20 +250,44 @@ def tile_moe_two_glu_relu_kernel(
                 result[:].indirect(slots_of(places, e)), y_copies[e][:], gates[:, e * C : (e + 1) * C], MULT
             )
 
-        calls = (
-            (multiply_a, 0),
-            (multiply_b, 0),
-            (rectify, 0),
-            (gate_hidden, 1),
-            (quantise_hidden, 3),
-            (turn, 2),
-            (empty_turned, 2),
-            (multiply_second, 3),
-            (send_back, 4),
-            (take_out, 3),
-        )
-        for step in range(E + max(lag for call, lag in calls)):
-            for call, lag in calls:
-                if 0 <= step - lag < E:
-                    call(step - lag)
+        multiply_a(0)
+        multiply_b(0)
+        rectify(0)
+        multiply_a(1)
+        multiply_b(1)
+        rectify(1)
+        gate_hidden(0)
+        turn(0)
+        empty_turned(0)
+        multiply_a(2)
+        rectify(2)
+        gate_hidden(1)
+        quantise_hidden(0)
+        turn(1)
+        empty_turned(1)
+        multiply_b(2)
+        gate_hidden(2)
+        multiply_a(3)
+        multiply_b(3)
+        rectify(3)
+        quantise_hidden(1)
+        gate_hidden(3)
+        multiply_second(0)
+        take_out(0)
+        turn(2)
+        empty_turned(2)
+        multiply_second(1)
+        take_out(1)
+        turn(3)
+        empty_turned(3)
+        send_back(0)
+        quantise_hidden(2)
+        multiply_second(2)
+        take_out(2)
+        send_back(1)
+        quantise_hidden(3)
+        multiply_second(3)
+        take_out(3)
+        send_back(2)
+        send_back(3)
         nc.sync.dma_start(out, result[:])

@@ -212,7 +212,7 @@ def tile_moe_two_glu_relu_kernel(
             return banks[TURNED_BANKS[e][g]][:].rearrange("p (g v c) -> p g v c", g=PASSES, v=2)
 
         def turn(e, first=0, last=PASSES):
-            for g in reversed(range(first, last)):
+            for g in range(first, last):
                 pairs = hidden[e][g][:].bitcast(F32)
                 for v in range(2):
                     nc.tensor.transpose(turned_bank(e, g)[:, g, v, :], pairs[:, v * P : (v + 1) * P], identity[:])

@@ -24,14 +24,14 @@ HALF = 512
 PASSES = H // HALF
 SCALE_ROWS = 16
 LIST_COLS = C // 16
-W2_FIRST = 2
 PAIR = 2
+WARM_UP_PASSES = 3
 
 A_BANKS = ((0, 1), (4, 5), (0, 1), (0, 1))
 B_BANKS = ((2, 3), (6, 7), (2, 3), (6, 7))
-TURNED_BANKS = ((4, 4), (5, 5), (0, 0), (1, 1))
+TURNED_BANKS = (4, 5, 0, 1)
 Y_BANKS = (2, 3, 4, 5)
-GATE_BANK = 7
+WARM_UP_BANK, GATE_BANK = B_BANKS[1]
 
 
 def tile_moe_two_glu_relu_kernel(
@@ -50,7 +50,8 @@ def tile_moe_two_glu_relu_kernel(
             return [keep.tile(shape, U8, name="%s%d" % (name, q), align_bytes=64) for q in range(E // PAIR)]
 
         def per_half(name, dtype):
-            return [[keep.tile([P, HALF], dtype, name="%s%d_%d" % (name, e, g), tag="%s%d_%d" % (name, e, g), align_bytes=64) for g in range(PASSES)] for e in range(E)]
+            names = [["%s%d_%d" % (name, e, g) for g in range(PASSES)] for e in range(E)]
+            return [[keep.tile([P, HALF], dtype, name=n, tag=n, align_bytes=64) for n in row] for row in names]
 
         sources = keep.tile([P, E * LIST_COLS], U16, name="sources")
         places = keep.tile([P, E * LIST_COLS], U16, name="places")
@@ -59,10 +60,8 @@ def tile_moe_two_glu_relu_kernel(
         gates = keep.tile([P, E * C], F32, name="gates")
         w1 = per_expert("w1_", [P, 2 * H], U8)
         w3 = per_expert("w3_", [P, 2 * H], U8)
-        w2_first = keep.tile([P, W2_FIRST * PASSES, 2 * N], U8, name="w2_first", align_bytes=64)
-        w2_rest = keep.tile([P, (E - W2_FIRST) * PASSES, 2 * N], U8, name="w2_rest", align_bytes=64)
-        s1_all = keep.tile([P, E, H], U8, name="s1", align_bytes=64)
-        s1 = [s1_all[:, :PAIR, :], s1_all[:, PAIR:, :]]
+        w2 = per_pair("w2_", [P, PAIR * PASSES, 2 * N])
+        s1 = keep.tile([P, E, H], U8, name="s1", align_bytes=64)
         s3 = per_pair("s3_", [P, PAIR, H])
         s2 = keep.tile([P, E * PASSES, N], U8, name="s2", align_bytes=64)
         identity = keep.tile([P, P], F32, name="identity")
@@ -70,14 +69,14 @@ def tile_moe_two_glu_relu_kernel(
         column = keep.tile([P, 1], F32, name="column")
         nc.gpsimd.memset(column[:], 0.0)
         nc.scalar.activation(column[:], column[:], RELU)
-        for scales in (s1_all, s3[0], s2, s3[1]):
+        for scales in (s1, s3[0], s2, s3[1]):
             nc.vector.memset(scales[:].bitcast(I32), 0)
         idle_codes = keep.tile([P, HALF], U32, name="idle_codes", align_bytes=64)
         idle_scales = keep.tile([P, HALF], U8, name="idle_scales", align_bytes=64)
         nc.vector.quantize_mx(
             out=idle_codes[:].bitcast(FP8X4),
             scales=idle_scales[:],
-            in_=s1_all[:].rearrange("p e i -> p (e i)").bitcast(BF16),
+            in_=s1[:].rearrange("p e i -> p (e i)").bitcast(BF16),
         )
         make_identity(nc, identity[:])
 
@@ -95,8 +94,9 @@ def tile_moe_two_glu_relu_kernel(
         def pair_of(tensor, q):
             return tensor[q * PAIR : (q + 1) * PAIR]
 
-        def load_second_words(tile, words):
-            nc.sync.dma_start(tile[:].bitcast(I32), words.bitcast(I32).rearrange("e s p c -> p (e s) c"))
+        def load_second_words(q):
+            words = pair_of(w2_words, q).bitcast(I32).rearrange("e s p c -> p (e s) c")
+            nc.sync.dma_start(w2[q][:].bitcast(I32), words)
 
         load_plane(0)
         nc.sync.dma_start(sources[:], offs)
@@ -106,28 +106,26 @@ def tile_moe_two_glu_relu_kernel(
         load_plane(3)
         load_words(w1, w1_words, 0)
         load_words(w3, w3_words, 0)
-        load_scales(nc.sync,s1_all[:],w1_scales)
+        load_scales(nc.sync, s1[:], w1_scales)
         load_scales(nc.sync, s3[0][:], pair_of(w3_scales, 0))
         load_scales(nc.gpsimd, s2[:], w2_scales)
-        load_words(w1, w1_words, 1)
-        load_words(w3, w3_words, 1)
-        load_words(w1, w1_words, 2)
-        load_scales(nc.sync, s3[1][:], pair_of(w3_scales, 1))
-        load_words(w3, w3_words, 2)
-        load_words(w1, w1_words, 3)
-        load_words(w3, w3_words, 3)
-        load_second_words(w2_first, w2_words[:W2_FIRST])
+        for e in range(1, E):
+            load_words(w1, w1_words, e)
+            if e % PAIR == 0:
+                load_scales(nc.sync, s3[e // PAIR][:], pair_of(w3_scales, e // PAIR))
+            load_words(w3, w3_words, e)
+        load_second_words(0)
         nc.sync.dma_start(places[:], dst)
-        load_second_words(w2_rest, w2_words[W2_FIRST:])
+        load_second_words(1)
 
         spread = banks[GATE_BANK][:].rearrange("n (u p) -> n u p", u=PACK)
         for u in range(PACK):
             nc.tensor.transpose(spread[:, u, :], gate_row[:, u : u + 1].to_broadcast([P, P]), identity[:])
         nc.scalar.copy(gates[:].rearrange("n (p u) -> n p u", u=PACK), spread.rearrange("n u p -> n p u"))
 
-        for repeat in range(3):
+        for repeat in range(WARM_UP_PASSES):
             nc.tensor.matmul_mx(
-                out=banks[6][:],
+                out=banks[WARM_UP_BANK][:],
                 lhsT=w1[0][:, : 2 * P].bitcast(FP4X4),
                 lhsT_scale=idle_scales[:, :P],
                 rhs=idle_codes[:].bitcast(FP8X4),
@@ -160,37 +158,37 @@ def tile_moe_two_glu_relu_kernel(
                 if t == 1 and e > 0:
                     quantise_tokens(e - 1)
         quantise_tokens(E - 1)
-        result = keep.tile([P, T], F32, name="result", tag="plane3")
+
+        result = keep.tile([P, T], F32, name="result", tag="plane%d" % (PACK - 1))
         nc.vector.memset(result[:], 0.0)
 
         relus = per_half("relu", F32)
         hidden = per_half("hidden", BF16)
         turned = per_expert("turned", [P, PASSES * C * PACK], BF16)
+        code_tags = ["hidden_codes0", "relu2_0", "hidden_codes2", "hidden_codes3"]
         hidden_codes = [
-            keep.tile([P, PASSES * C], U32, name="hidden_codes%d" % e, align_bytes=64, tag="relu2_0" if e == 1 else "hidden_codes%d" % e)
-            for e in range(E)
+            keep.tile([P, PASSES * C], U32, name="hidden_codes%d" % e, align_bytes=64, tag=code_tags[e]) for e in range(E)
         ]
         hidden_scales = per_expert("hidden_scales", [P, PASSES * C], U8)
         y_copies = per_expert("y_copy", [P, C], F32)
 
-        def multiply_first(e, g, bank, words, scales):
-            nc.tensor.matmul_mx(
-                out=bank[:],
-                lhsT=token_codes[e][:].bitcast(FP8X4),
-                lhsT_scale=token_scales[e][:],
-                rhs=words[e][:, 2 * g * HALF : 2 * (g + 1) * HALF].bitcast(FP4X4),
-                rhs_scale=scales[e // PAIR][:, e % PAIR, g * HALF : (g + 1) * HALF],
-                start=True,
-                stop=True,
-            )
+        def multiply_first(e, bank_numbers, words, scales):
+            for g in range(PASSES):
+                nc.tensor.matmul_mx(
+                    out=banks[bank_numbers[g]][:],
+                    lhsT=token_codes[e][:].bitcast(FP8X4),
+                    lhsT_scale=token_scales[e][:],
+                    rhs=words[:, 2 * g * HALF : 2 * (g + 1) * HALF].bitcast(FP4X4),
+                    rhs_scale=scales[:, g * HALF : (g + 1) * HALF],
+                    start=True,
+                    stop=True,
+                )
 
         def multiply_a(e):
-            for g in range(PASSES):
-                multiply_first(e, g, banks[A_BANKS[e][g]], w1, s1)
+            multiply_first(e, A_BANKS[e], w1[e], s1[:, e, :])
 
         def multiply_b(e):
-            for g in range(PASSES):
-                multiply_first(e, g, banks[B_BANKS[e][g]], w3, s3)
+            multiply_first(e, B_BANKS[e], w3[e], s3[e // PAIR][:, e % PAIR, :])
 
         def bank_order(bank):
             return bank[:].rearrange("s (m v d) -> s v m d", v=2, d=2)
@@ -208,33 +206,29 @@ def tile_moe_two_glu_relu_kernel(
                     pair_order(hidden[e][g]), bank_order(banks[B_BANKS[e][g]]), pair_order(relus[e][g]), MULT
                 )
 
-        def turned_bank(e, g):
-            return banks[TURNED_BANKS[e][g]][:].rearrange("p (g v c) -> p g v c", g=PASSES, v=2)
+        def turned_bank(e):
+            return banks[TURNED_BANKS[e]][:].rearrange("p (g v c) -> p g v c", g=PASSES, v=2)
 
-        def turn(e, first=0, last=PASSES):
-            for g in range(first, last):
+        def turn(e):
+            for g in range(PASSES):
                 pairs = hidden[e][g][:].bitcast(F32)
                 for v in range(2):
-                    nc.tensor.transpose(turned_bank(e, g)[:, g, v, :], pairs[:, v * P : (v + 1) * P], identity[:])
+                    nc.tensor.transpose(turned_bank(e)[:, g, v, :], pairs[:, v * P : (v + 1) * P], identity[:])
 
-        def empty_turned(e, first=0, last=PASSES):
+        def empty_turned(e):
             nc.scalar.copy(
-                turned[e][:].bitcast(F32).rearrange("p (g c v) -> p g c v", g=PASSES, v=2)[:, first:last],
-                turned_bank(e, first).rearrange("p g v c -> p g c v")[:, first:last],
+                turned[e][:].bitcast(F32).rearrange("p (g c v) -> p g c v", g=PASSES, v=2),
+                turned_bank(e).rearrange("p g v c -> p g c v"),
             )
 
-        def quantise_hidden(e, first=0, last=PASSES):
-            nc.vector.quantize_mx(
-                out=hidden_codes[e][:, first * C : last * C].bitcast(FP8X4),
-                scales=hidden_scales[e][:, first * C : last * C],
-                in_=turned[e][:, first * C * PACK : last * C * PACK],
-            )
+        def quantise_hidden(e):
+            nc.vector.quantize_mx(out=hidden_codes[e][:].bitcast(FP8X4), scales=hidden_scales[e][:], in_=turned[e][:])
 
         def multiply_second(e):
             for g in range(PASSES):
                 nc.tensor.matmul_mx(
                     out=banks[Y_BANKS[e]][:, :C],
-                    lhsT=(w2_first[:, e * PASSES + g, :] if e < W2_FIRST else w2_rest[:, (e - W2_FIRST) * PASSES + g, :]).bitcast(FP4X4),
+                    lhsT=w2[e // PAIR][:, (e % PAIR) * PASSES + g, :].bitcast(FP4X4),
                     lhsT_scale=s2[:, e * PASSES + g, :],
                     rhs=hidden_codes[e][:, g * C : (g + 1) * C].bitcast(FP8X4),
                     rhs_scale=hidden_scales[e][:, g * C : (g + 1) * C],
@@ -250,44 +244,14 @@ def tile_moe_two_glu_relu_kernel(
                 result[:].indirect(slots_of(places, e)), y_copies[e][:], gates[:, e * C : (e + 1) * C], MULT
             )
 
-        multiply_a(0)
-        multiply_b(0)
-        rectify(0)
-        multiply_a(1)
-        multiply_b(1)
-        rectify(1)
-        gate_hidden(0)
-        turn(0)
-        empty_turned(0)
-        multiply_a(2)
-        rectify(2)
-        gate_hidden(1)
-        quantise_hidden(0)
-        turn(1)
-        empty_turned(1)
-        multiply_b(2)
-        gate_hidden(2)
-        multiply_a(3)
-        multiply_b(3)
-        rectify(3)
-        quantise_hidden(1)
-        gate_hidden(3)
-        multiply_second(0)
-        take_out(0)
-        turn(2)
-        empty_turned(2)
-        multiply_second(1)
-        take_out(1)
-        turn(3)
-        empty_turned(3)
-        send_back(0)
-        quantise_hidden(2)
-        multiply_second(2)
-        take_out(2)
-        send_back(1)
-        quantise_hidden(3)
-        multiply_second(3)
-        take_out(3)
-        send_back(2)
-        send_back(3)
+        stages = (
+            (4, (multiply_second, take_out, send_back)),
+            (2, (turn, empty_turned, quantise_hidden)),
+            (0, (multiply_a, multiply_b, rectify, gate_hidden)),
+        )
+        for step in range(E + stages[0][0]):
+            for lag, calls in stages:
+                if 0 <= step - lag < E:
+                    for call in calls:
+                        call(step - lag)
         nc.sync.dma_start(out, result[:])

@@ -57,7 +57,6 @@ def tile_moe_two_glu_relu_kernel(
         places = keep.tile([P, E * LIST_COLS], U16, name="places")
         planes = [keep.tile([P, T], F32, name="plane%d" % t, tag="plane%d" % t) for t in range(PACK)]
         gate_row = keep.tile([P, PACK], F32, name="gate_row")
-        gates = keep.tile([P, E * C], F32, name="gates")
         w1 = per_expert("w1_", [P, 2 * H], U8)
         w3 = per_expert("w3_", [P, 2 * H], U8)
         w2 = per_pair("w2_", [P, PAIR * PASSES, 2 * N])
@@ -68,16 +67,10 @@ def tile_moe_two_glu_relu_kernel(
 
         column = keep.tile([P, 1], F32, name="column")
         nc.gpsimd.memset(column[:], 0.0)
-        nc.scalar.activation(column[:], column[:], RELU)
+        result = keep.tile([P, T], F32, name="result")
+        nc.scalar.activation(result[:], column[:].to_broadcast([P, T]), RELU)
         for scales in (s1, s3[0], s2, s3[1]):
             nc.vector.memset(scales[:].bitcast(I32), 0)
-        idle_codes = keep.tile([P, HALF], U32, name="idle_codes", align_bytes=64)
-        idle_scales = keep.tile([P, HALF], U8, name="idle_scales", align_bytes=64)
-        nc.vector.quantize_mx(
-            out=idle_codes[:].bitcast(FP8X4),
-            scales=idle_scales[:],
-            in_=s1[:].rearrange("p e i -> p (e i)").bitcast(BF16),
-        )
         make_identity(nc, identity[:])
 
         def load_plane(t):
@@ -121,18 +114,6 @@ def tile_moe_two_glu_relu_kernel(
         spread = banks[GATE_BANK][:].rearrange("n (u p) -> n u p", u=PACK)
         for u in range(PACK):
             nc.tensor.transpose(spread[:, u, :], gate_row[:, u : u + 1].to_broadcast([P, P]), identity[:])
-        nc.scalar.copy(gates[:].rearrange("n (p u) -> n p u", u=PACK), spread.rearrange("n u p -> n p u"))
-
-        for repeat in range(WARM_UP_PASSES):
-            nc.tensor.matmul_mx(
-                out=banks[WARM_UP_BANK][:],
-                lhsT=w1[0][:, : 2 * P].bitcast(FP4X4),
-                lhsT_scale=idle_scales[:, :P],
-                rhs=idle_codes[:].bitcast(FP8X4),
-                rhs_scale=idle_scales[:],
-                start=True,
-                stop=True,
-            )
 
         rounded = [keep.tile([P, T], BF16, name="rounded%d" % t, align_bytes=64) for t in range(2)]
         tokens = per_expert("tokens", [P, C, PACK], BF16)
@@ -149,8 +130,34 @@ def tile_moe_two_glu_relu_kernel(
                 in_=tokens[e][:].rearrange("p c t -> p (c t)"),
             )
 
+        idle_codes = keep.tile([P, HALF], U32, name="idle_codes", align_bytes=64)
+        idle_scales = keep.tile([P, HALF], U8, name="idle_scales", align_bytes=64)
+
+        def warm_up():
+            width = T // PACK
+            for start in range(0, HALF, width):
+                nc.vector.quantize_mx(
+                    out=idle_codes[:, start : start + width].bitcast(FP8X4),
+                    scales=idle_scales[:, start : start + width],
+                    in_=rounded[0][:],
+                )
+            for repeat in range(WARM_UP_PASSES):
+                nc.tensor.matmul_mx(
+                    out=banks[WARM_UP_BANK][:],
+                    lhsT=w1[0][:, : 2 * P].bitcast(FP4X4),
+                    lhsT_scale=idle_scales[:, :P],
+                    rhs=idle_codes[:].bitcast(FP8X4),
+                    rhs_scale=idle_scales[:],
+                    start=True,
+                    stop=True,
+                )
+
         for t in range(2):
-            nc.vector.tensor_copy(rounded[t][:], planes[t][:])
+            if t == 0:
+                nc.vector.tensor_copy(rounded[t][:], planes[t][:])
+                warm_up()
+            else:
+                nc.scalar.activation(rounded[t][:], planes[t][:], COPY)
             for e in range(E):
                 nc.scalar.activation(tokens[e][:, :, t], rounded[t][:].indirect(slots_of(sources, e)), COPY)
             for e in range(E):
@@ -159,8 +166,8 @@ def tile_moe_two_glu_relu_kernel(
                     quantise_tokens(e - 1)
         quantise_tokens(E - 1)
 
-        result = keep.tile([P, T], F32, name="result", tag="plane%d" % (PACK - 1))
-        nc.vector.memset(result[:], 0.0)
+        gates = keep.tile([P, E * C], F32, name="gates", tag="plane%d" % (PACK - 1))
+        nc.vector.tensor_copy(gates[:].rearrange("n (p u) -> n p u", u=PACK), spread.rearrange("n u p -> n p u"))
 
         relus = per_half("relu", F32)
         hidden = per_half("hidden", BF16)

@@ -25,7 +25,7 @@ PASSES = H // HALF
 SCALE_ROWS = 16
 LIST_COLS = C // 16
 PAIR = 2
-WARM_UP_PASSES = 3
+WARM_UP_PASSES = 2
 
 A_BANKS = ((0, 1), (4, 5), (0, 1), (0, 1))
 B_BANKS = ((2, 3), (6, 7), (2, 3), (6, 7))
@@ -98,9 +98,9 @@ def tile_moe_two_glu_relu_kernel(
         load_plane(1)
         load_plane(3)
         load_words(w1, w1_words, 0)
-        load_words(w3, w3_words, 0)
         load_scales(nc.sync, s1[:], w1_scales)
         load_scales(nc.sync, s3[0][:], pair_of(w3_scales, 0))
+        load_words(w3, w3_words, 0)
         load_scales(nc.gpsimd, s2[:], w2_scales)
         for e in range(1, E):
             load_words(w1, w1_words, e)

@@ -29,7 +29,7 @@ WARM_UP_PASSES = 2
 
 A_BANKS = ((0, 1), (4, 5), (0, 1), (0, 1))
 B_BANKS = ((2, 3), (6, 7), (2, 3), (6, 7))
-TURNED_BANKS = (4, 5, 0, 1)
+TURNED_PLACES = (((4, 0), (4, 1)), ((5, 0), (5, 1)), ((3, 1), (0, 1)), ((2, 0), (2, 1)))
 Y_BANKS = (2, 3, 4, 5)
 WARM_UP_BANK, GATE_BANK = B_BANKS[1]
 
@@ -69,7 +69,7 @@ def tile_moe_two_glu_relu_kernel(
         nc.gpsimd.memset(column[:], 0.0)
         result = keep.tile([P, T], F32, name="result")
         nc.scalar.activation(result[:], column[:].to_broadcast([P, T]), RELU)
-        for scales in (s1, s3[0], s2, s3[1]):
+        for scales in (s1, s3[0], s3[1], s2):
             nc.vector.memset(scales[:].bitcast(I32), 0)
         make_identity(nc, identity[:])
 
@@ -101,14 +101,14 @@ def tile_moe_two_glu_relu_kernel(
         load_scales(nc.sync, s1[:], w1_scales)
         load_scales(nc.sync, s3[0][:], pair_of(w3_scales, 0))
         load_words(w3, w3_words, 0)
-        load_scales(nc.gpsimd, s2[:], w2_scales)
         for e in range(1, E):
             load_words(w1, w1_words, e)
             if e % PAIR == 0:
                 load_scales(nc.sync, s3[e // PAIR][:], pair_of(w3_scales, e // PAIR))
             load_words(w3, w3_words, e)
-        load_second_words(0)
+        load_scales(nc.sync, s2[:], w2_scales)
         nc.sync.dma_start(places[:], dst)
+        load_second_words(0)
         load_second_words(1)
 
         spread = banks[GATE_BANK][:].rearrange("n (u p) -> n u p", u=PACK)
@@ -213,20 +213,28 @@ def tile_moe_two_glu_relu_kernel(
                     pair_order(hidden[e][g]), bank_order(banks[B_BANKS[e][g]]), pair_order(relus[e][g]), MULT
                 )
 
-        def turned_bank(e):
-            return banks[TURNED_BANKS[e]][:].rearrange("p (g v c) -> p g v c", g=PASSES, v=2)
+        def bank_halves(number):
+            return banks[number][:].rearrange("p (g v c) -> p g v c", g=PASSES, v=2)
+
+        def turn_half(e, g):
+            number, place = TURNED_PLACES[e][g]
+            pairs = hidden[e][g][:].bitcast(F32)
+            for v in range(2):
+                nc.tensor.transpose(bank_halves(number)[:, place, v, :], pairs[:, v * P : (v + 1) * P], identity[:])
 
         def turn(e):
             for g in range(PASSES):
-                pairs = hidden[e][g][:].bitcast(F32)
-                for v in range(2):
-                    nc.tensor.transpose(turned_bank(e)[:, g, v, :], pairs[:, v * P : (v + 1) * P], identity[:])
+                turn_half(e, g)
+
+        def turned_words(e):
+            return turned[e][:].bitcast(F32).rearrange("p (g c v) -> p g c v", g=PASSES, v=2)
+
+        def empty_half(e, g):
+            number, place = TURNED_PLACES[e][g]
+            nc.scalar.copy(turned_words(e)[:, g], bank_halves(number)[:, place].rearrange("p v c -> p c v"))
 
         def empty_turned(e):
-            nc.scalar.copy(
-                turned[e][:].bitcast(F32).rearrange("p (g c v) -> p g c v", g=PASSES, v=2),
-                turned_bank(e).rearrange("p g v c -> p g c v"),
-            )
+            nc.scalar.copy(turned_words(e), bank_halves(TURNED_PLACES[e][0][0]).rearrange("p g v c -> p g c v"))
 
         def quantise_hidden(e):
             nc.vector.quantize_mx(out=hidden_codes[e][:].bitcast(FP8X4), scales=hidden_scales[e][:], in_=turned[e][:])
@@ -251,14 +259,29 @@ def tile_moe_two_glu_relu_kernel(
                 result[:].indirect(slots_of(places, e)), y_copies[e][:], gates[:, e * C : (e + 1) * C], MULT
             )
 
-        stages = (
-            (4, (multiply_second, take_out, send_back)),
-            (2, (turn, empty_turned, quantise_hidden)),
-            (0, (multiply_a, multiply_b, rectify, gate_hidden)),
-        )
-        for step in range(E + stages[0][0]):
-            for lag, calls in stages:
-                if 0 <= step - lag < E:
-                    for call in calls:
-                        call(step - lag)
+        def run(calls, e):
+            for call in calls:
+                call(e)
+
+        first_layer = (multiply_a, multiply_b, rectify, gate_hidden)
+        to_codes = (turn, empty_turned, quantise_hidden)
+        second_layer = (multiply_second, take_out, send_back)
+        run(first_layer, 0)
+        run(first_layer, 1)
+        run(to_codes, 0)
+        run(first_layer, 2)
+        run(to_codes, 1)
+        run(first_layer, 3)
+        turn_half(2, 1)
+        empty_half(2, 1)
+        run(second_layer, 0)
+        multiply_second(1)
+        turn_half(2, 0)
+        empty_half(2, 0)
+        quantise_hidden(2)
+        take_out(1)
+        send_back(1)
+        run(to_codes, 3)
+        run(second_layer, 2)
+        run(second_layer, 3)
         nc.sync.dma_start(out, result[:])

@@ -25,12 +25,13 @@ PASSES = H // HALF
 SCALE_ROWS = 16
 LIST_COLS = C // 16
 PAIR = 2
+LAST = E - 1
 WARM_UP_PASSES = 2
 
 A_BANKS = ((0, 1), (4, 5), (0, 1), (0, 1))
 B_BANKS = ((2, 3), (6, 7), (2, 3), (6, 7))
-TURNED_PLACES = (((4, 0), (4, 1)), ((5, 0), (5, 1)), ((3, 1), (0, 1)), ((2, 0), (2, 1)))
 Y_BANKS = (2, 3, 4, 5)
+TURNED_PLACES = (((4, 0), (4, 1)), ((5, 0), (5, 1)), ((2, 1), (3, 1)), ((2, 0), (0, 1)))
 WARM_UP_BANK, GATE_BANK = B_BANKS[1]
 
 
@@ -43,11 +44,8 @@ def tile_moe_two_glu_relu_kernel(
         psum = ctx.enter_context(tc.psum_pool(name="psum", bufs=1))
         banks = [psum.tile([P, HALF], F32, name="bank%d" % n) for n in range(8)]
 
-        def per_expert(name, shape, dtype):
-            return [keep.tile(shape, dtype, name="%s%d" % (name, e), align_bytes=64) for e in range(E)]
-
-        def per_pair(name, shape):
-            return [keep.tile(shape, U8, name="%s%d" % (name, q), align_bytes=64) for q in range(E // PAIR)]
+        def per_expert(name, shape, dtype, experts=range(E)):
+            return [keep.tile(shape, dtype, name="%s%d" % (name, e), align_bytes=64) for e in experts]
 
         def per_half(name, dtype):
             names = [["%s%d_%d" % (name, e, g) for g in range(PASSES)] for e in range(E)]
@@ -58,15 +56,17 @@ def tile_moe_two_glu_relu_kernel(
         planes = [keep.tile([P, T], F32, name="plane%d" % t, tag="plane%d" % t) for t in range(PACK)]
         gate_row = keep.tile([P, PACK], F32, name="gate_row")
         w1 = per_expert("w1_", [P, 2 * H], U8)
-        w3 = per_expert("w3_", [P, 2 * H], U8)
-        w2 = per_pair("w2_", [P, PAIR * PASSES, 2 * N])
+        w3 = per_expert("w3_", [P, 2 * H], U8, range(LAST))
+        w3_last = per_expert("w3_last", [P, 2 * HALF], U8, range(PASSES))
+        w2_early = per_expert("w2_", [P, PASSES, 2 * N], U8, range(PAIR))
+        w2_late = keep.tile([P, PAIR * PASSES, 2 * N], U8, name="w2_late", align_bytes=64)
         s1 = keep.tile([P, E, H], U8, name="s1", align_bytes=64)
-        s3 = per_pair("s3_", [P, PAIR, H])
+        s3 = per_expert("s3_", [P, PAIR, H], U8, range(E // PAIR))
         s2 = keep.tile([P, E * PASSES, N], U8, name="s2", align_bytes=64)
         identity = keep.tile([P, P], F32, name="identity")
 
         column = keep.tile([P, 1], F32, name="column")
-        nc.gpsimd.memset(column[:], 0.0)
+        nc.vector.memset(column[:], 0.0)
         result = keep.tile([P, T], F32, name="result")
         nc.scalar.activation(result[:], column[:].to_broadcast([P, T]), RELU)
         for scales in (s1, s3[0], s3[1], s2):
@@ -76,20 +76,20 @@ def tile_moe_two_glu_relu_kernel(
         def load_plane(t):
             nc.sync.dma_start(planes[t][:], xT.rearrange("(p t) n -> p t n", t=PACK)[:, t, :])
 
-        def load_words(tiles, words, e):
-            nc.sync.dma_start(tiles[e][:].bitcast(I32), words[e, 0].bitcast(I32))
+        def load_raw(into, source):
+            nc.sync.dma_start(into.bitcast(I32), source.bitcast(I32))
 
-        def load_scales(queue, into, rows):
+        def load_scales(into, rows):
             rows = rows.bitcast(I32).rearrange("e s q c -> q (e s) c")
             for r in range(4):
-                queue.dma_start(into.bitcast(I32)[r:P:32, :, :], rows[r:SCALE_ROWS:4, :, :])
+                nc.sync.dma_start(into.bitcast(I32)[r:P:32, :, :], rows[r:SCALE_ROWS:4, :, :])
 
-        def pair_of(tensor, q):
-            return tensor[q * PAIR : (q + 1) * PAIR]
+        def load_second(into, first, count):
+            words = w2_words[first : first + count].bitcast(I32).rearrange("e s p c -> p (e s) c")
+            nc.sync.dma_start(into[:].bitcast(I32), words)
 
-        def load_second_words(q):
-            words = pair_of(w2_words, q).bitcast(I32).rearrange("e s p c -> p (e s) c")
-            nc.sync.dma_start(w2[q][:].bitcast(I32), words)
+        def load_last_half(g):
+            load_raw(w3_last[g][:], w3_words[LAST, 0][:, 2 * g * HALF : 2 * (g + 1) * HALF])
 
         load_plane(0)
         nc.sync.dma_start(sources[:], offs)
@@ -97,19 +97,23 @@ def tile_moe_two_glu_relu_kernel(
         load_plane(2)
         load_plane(1)
         load_plane(3)
-        load_words(w1, w1_words, 0)
-        load_scales(nc.sync, s1[:], w1_scales)
-        load_scales(nc.sync, s3[0][:], pair_of(w3_scales, 0))
-        load_words(w3, w3_words, 0)
-        for e in range(1, E):
-            load_words(w1, w1_words, e)
-            if e % PAIR == 0:
-                load_scales(nc.sync, s3[e // PAIR][:], pair_of(w3_scales, e // PAIR))
-            load_words(w3, w3_words, e)
-        load_scales(nc.sync, s2[:], w2_scales)
+        load_raw(w1[0][:], w1_words[0, 0])
+        load_scales(s1[:], w1_scales)
+        load_scales(s3[0][:], w3_scales[:PAIR])
+        load_raw(w3[0][:], w3_words[0, 0])
+        for e in range(1, LAST):
+            load_raw(w1[e][:], w1_words[e, 0])
+            if e == PAIR:
+                load_scales(s3[1][:], w3_scales[PAIR:])
+            load_raw(w3[e][:], w3_words[e, 0])
+        load_raw(w1[LAST][:], w1_words[LAST, 0])
+        load_last_half(0)
+        load_scales(s2[:], w2_scales)
+        load_second(w2_early[0], 0, 1)
+        load_last_half(1)
+        load_second(w2_early[1], 1, 1)
         nc.sync.dma_start(places[:], dst)
-        load_second_words(0)
-        load_second_words(1)
+        load_second(w2_late, PAIR, PAIR)
 
         spread = banks[GATE_BANK][:].rearrange("n (u p) -> n u p", u=PACK)
         for u in range(PACK):
@@ -164,9 +168,9 @@ def tile_moe_two_glu_relu_kernel(
                 nc.vector.tensor_copy(tokens[e][:, :, t + 2], planes[t + 2][:].indirect(slots_of(sources, e)))
                 if t == 1 and e > 0:
                     quantise_tokens(e - 1)
-        quantise_tokens(E - 1)
+        quantise_tokens(LAST)
 
-        gates = keep.tile([P, E * C], F32, name="gates", tag="plane%d" % (PACK - 1))
+        gates = keep.tile([P, E * C], F32, name="gates")
         nc.vector.tensor_copy(gates[:].rearrange("n (p u) -> n p u", u=PACK), spread.rearrange("n u p -> n p u"))
 
         relus = per_half("relu", F32)
@@ -177,25 +181,25 @@ def tile_moe_two_glu_relu_kernel(
             keep.tile([P, PASSES * C], U32, name="hidden_codes%d" % e, align_bytes=64, tag=code_tags[e]) for e in range(E)
         ]
         hidden_scales = per_expert("hidden_scales", [P, PASSES * C], U8)
-        y_copies = per_expert("y_copy", [P, C], F32)
+        gated = per_expert("gated", [P, C], F32)
 
-        def multiply_first(e, bank_numbers, words, scales):
-            for g in range(PASSES):
-                nc.tensor.matmul_mx(
-                    out=banks[bank_numbers[g]][:],
-                    lhsT=token_codes[e][:].bitcast(FP8X4),
-                    lhsT_scale=token_scales[e][:],
-                    rhs=words[:, 2 * g * HALF : 2 * (g + 1) * HALF].bitcast(FP4X4),
-                    rhs_scale=scales[:, g * HALF : (g + 1) * HALF],
-                    start=True,
-                    stop=True,
-                )
+        def multiply_first(e, g, bank, words, scales):
+            nc.tensor.matmul_mx(
+                out=banks[bank][:],
+                lhsT=token_codes[e][:].bitcast(FP8X4),
+                lhsT_scale=token_scales[e][:],
+                rhs=words.bitcast(FP4X4),
+                rhs_scale=scales[:, g * HALF : (g + 1) * HALF],
+                start=True,
+                stop=True,
+            )
 
-        def multiply_a(e):
-            multiply_first(e, A_BANKS[e], w1[e], s1[:, e, :])
+        def multiply_a(e, g):
+            multiply_first(e, g, A_BANKS[e][g], w1[e][:, 2 * g * HALF : 2 * (g + 1) * HALF], s1[:, e, :])
 
-        def multiply_b(e):
-            multiply_first(e, B_BANKS[e], w3[e], s3[e // PAIR][:, e % PAIR, :])
+        def multiply_b(e, g):
+            words = w3_last[g][:] if e == LAST else w3[e][:, 2 * g * HALF : 2 * (g + 1) * HALF]
+            multiply_first(e, g, B_BANKS[e][g], words, s3[e // PAIR][:, e % PAIR, :])
 
         def bank_order(bank):
             return bank[:].rearrange("s (m v d) -> s v m d", v=2, d=2)
@@ -203,47 +207,43 @@ def tile_moe_two_glu_relu_kernel(
         def pair_order(tile):
             return tile[:].rearrange("s (v m d) -> s v m d", v=2, d=2)
 
-        def rectify(e):
-            for g in range(PASSES):
-                nc.scalar.activation(pair_order(relus[e][g]), bank_order(banks[A_BANKS[e][g]]), RELU)
+        def rectify(e, g):
+            nc.scalar.activation(pair_order(relus[e][g]), bank_order(banks[A_BANKS[e][g]]), RELU)
 
-        def gate_hidden(e):
-            for g in range(PASSES):
-                nc.vector.tensor_tensor(
-                    pair_order(hidden[e][g]), bank_order(banks[B_BANKS[e][g]]), pair_order(relus[e][g]), MULT
-                )
+        def gate_hidden(e, g):
+            nc.vector.tensor_tensor(
+                pair_order(hidden[e][g]), bank_order(banks[B_BANKS[e][g]]), pair_order(relus[e][g]), MULT
+            )
 
-        def bank_halves(number):
-            return banks[number][:].rearrange("p (g v c) -> p g v c", g=PASSES, v=2)
+        def sides(bank):
+            return banks[bank][:].rearrange("p (side v c) -> p side v c", side=2, v=2)
 
-        def turn_half(e, g):
-            number, place = TURNED_PLACES[e][g]
+        def turn(e, g):
+            bank, side = TURNED_PLACES[e][g]
             pairs = hidden[e][g][:].bitcast(F32)
             for v in range(2):
-                nc.tensor.transpose(bank_halves(number)[:, place, v, :], pairs[:, v * P : (v + 1) * P], identity[:])
-
-        def turn(e):
-            for g in range(PASSES):
-                turn_half(e, g)
+                nc.tensor.transpose(sides(bank)[:, side, v, :], pairs[:, v * P : (v + 1) * P], identity[:])
 
         def turned_words(e):
             return turned[e][:].bitcast(F32).rearrange("p (g c v) -> p g c v", g=PASSES, v=2)
 
-        def empty_half(e, g):
-            number, place = TURNED_PLACES[e][g]
-            nc.scalar.copy(turned_words(e)[:, g], bank_halves(number)[:, place].rearrange("p v c -> p c v"))
+        def empty_both(e):
+            nc.scalar.copy(turned_words(e), sides(TURNED_PLACES[e][0][0]).rearrange("p g v c -> p g c v"))
 
-        def empty_turned(e):
-            nc.scalar.copy(turned_words(e), bank_halves(TURNED_PLACES[e][0][0]).rearrange("p g v c -> p g c v"))
+        def empty_half(e, g):
+            bank, side = TURNED_PLACES[e][g]
+            copy = nc.scalar.copy if g == 0 else nc.vector.tensor_copy
+            copy(turned_words(e)[:, g], sides(bank)[:, side].rearrange("p v c -> p c v"))
 
         def quantise_hidden(e):
             nc.vector.quantize_mx(out=hidden_codes[e][:].bitcast(FP8X4), scales=hidden_scales[e][:], in_=turned[e][:])
 
         def multiply_second(e):
             for g in range(PASSES):
+                words = w2_early[e][:, g, :] if e < PAIR else w2_late[:, (e - PAIR) * PASSES + g, :]
                 nc.tensor.matmul_mx(
                     out=banks[Y_BANKS[e]][:, :C],
-                    lhsT=w2[e // PAIR][:, (e % PAIR) * PASSES + g, :].bitcast(FP4X4),
+                    lhsT=words.bitcast(FP4X4),
                     lhsT_scale=s2[:, e * PASSES + g, :],
                     rhs=hidden_codes[e][:, g * C : (g + 1) * C].bitcast(FP8X4),
                     rhs_scale=hidden_scales[e][:, g * C : (g + 1) * C],
@@ -252,36 +252,53 @@ def tile_moe_two_glu_relu_kernel(
                 )
 
         def take_out(e):
-            nc.scalar.copy(y_copies[e][:], banks[Y_BANKS[e]][:, :C])
+            nc.vector.tensor_tensor(gated[e][:], banks[Y_BANKS[e]][:, :C], gates[:, e * C : (e + 1) * C], MULT)
 
         def send_back(e):
-            nc.vector.tensor_tensor(
-                result[:].indirect(slots_of(places, e)), y_copies[e][:], gates[:, e * C : (e + 1) * C], MULT
-            )
+            nc.scalar.activation(result[:].indirect(slots_of(places, e)), gated[e][:], COPY)
 
-        def run(calls, e):
-            for call in calls:
-                call(e)
+        def first_layer(e):
+            for call in (multiply_a, multiply_b, rectify, gate_hidden):
+                for g in range(PASSES):
+                    call(e, g)
 
-        first_layer = (multiply_a, multiply_b, rectify, gate_hidden)
-        to_codes = (turn, empty_turned, quantise_hidden)
-        second_layer = (multiply_second, take_out, send_back)
-        run(first_layer, 0)
-        run(first_layer, 1)
-        run(to_codes, 0)
-        run(first_layer, 2)
-        run(to_codes, 1)
-        run(first_layer, 3)
-        turn_half(2, 1)
-        empty_half(2, 1)
-        run(second_layer, 0)
-        multiply_second(1)
-        turn_half(2, 0)
+        def to_codes(e):
+            for g in range(PASSES):
+                turn(e, g)
+            empty_both(e)
+            quantise_hidden(e)
+
+        first_layer(0)
+        first_layer(1)
+        to_codes(0)
+        first_layer(2)
+        to_codes(1)
+        for g in range(PASSES):
+            multiply_a(LAST, g)
+        multiply_b(LAST, 0)
+        for g in range(PASSES):
+            rectify(LAST, g)
+        gate_hidden(LAST, 0)
+        multiply_second(0)
+        turn(2, 0)
+        take_out(0)
         empty_half(2, 0)
-        quantise_hidden(2)
+        send_back(0)
+        multiply_b(LAST, 1)
+        gate_hidden(LAST, 1)
+        multiply_second(1)
+        turn(2, 1)
+        empty_half(2, 1)
         take_out(1)
+        quantise_hidden(2)
+        turn(LAST, 0)
+        empty_half(LAST, 0)
         send_back(1)
-        run(to_codes, 3)
-        run(second_layer, 2)
-        run(second_layer, 3)
+        turn(LAST, 1)
+        empty_half(LAST, 1)
+        quantise_hidden(LAST)
+        for e in range(PAIR, E):
+            multiply_second(e)
+            take_out(e)
+            send_back(e)
         nc.sync.dma_start(out, result[:])

@@ -31,7 +31,7 @@ WARM_UP_PASSES = 2
 A_BANKS = ((0, 1), (4, 5), (0, 1), (0, 1))
 B_BANKS = ((2, 3), (6, 7), (2, 3), (6, 7))
 Y_BANKS = (2, 3, 4, 5)
-TURNED_PLACES = (((4, 0), (4, 1)), ((5, 0), (5, 1)), ((2, 1), (3, 1)), ((2, 0), (0, 1)))
+TURNED_PLACES = (((4, 0), (4, 1)), ((5, 0), (5, 1)), ((3, 1), (0, 1)), ((2, 0), (3, 1)))
 WARM_UP_BANK, GATE_BANK = B_BANKS[1]
 
 
@@ -56,10 +56,9 @@ def tile_moe_two_glu_relu_kernel(
         planes = [keep.tile([P, T], F32, name="plane%d" % t, tag="plane%d" % t) for t in range(PACK)]
         gate_row = keep.tile([P, PACK], F32, name="gate_row")
         w1 = per_expert("w1_", [P, 2 * H], U8)
-        w3 = per_expert("w3_", [P, 2 * H], U8, range(LAST))
-        w3_last = per_expert("w3_last", [P, 2 * HALF], U8, range(PASSES))
-        w2_early = per_expert("w2_", [P, PASSES, 2 * N], U8, range(PAIR))
-        w2_late = keep.tile([P, PAIR * PASSES, 2 * N], U8, name="w2_late", align_bytes=64)
+        w3_tags = ["w3_0", "w3_1", "w3_0", "w3_3"]
+        w3 = [keep.tile([P, 2 * H], U8, name="w3_%d" % e, tag=w3_tags[e], align_bytes=64) for e in range(E)]
+        w2 = per_expert("w2_", [P, PAIR * PASSES, 2 * N], U8, range(E // PAIR))
         s1 = keep.tile([P, E, H], U8, name="s1", align_bytes=64)
         s3 = per_expert("s3_", [P, PAIR, H], U8, range(E // PAIR))
         s2 = keep.tile([P, E * PASSES, N], U8, name="s2", align_bytes=64)
@@ -84,12 +83,9 @@ def tile_moe_two_glu_relu_kernel(
             for r in range(4):
                 nc.sync.dma_start(into.bitcast(I32)[r:P:32, :, :], rows[r:SCALE_ROWS:4, :, :])
 
-        def load_second(into, first, count):
-            words = w2_words[first : first + count].bitcast(I32).rearrange("e s p c -> p (e s) c")
-            nc.sync.dma_start(into[:].bitcast(I32), words)
-
-        def load_last_half(g):
-            load_raw(w3_last[g][:], w3_words[LAST, 0][:, 2 * g * HALF : 2 * (g + 1) * HALF])
+        def load_second(q):
+            words = w2_words[q * PAIR : (q + 1) * PAIR].bitcast(I32).rearrange("e s p c -> p (e s) c")
+            nc.sync.dma_start(w2[q][:].bitcast(I32), words)
 
         load_plane(0)
         nc.sync.dma_start(sources[:], offs)
@@ -101,19 +97,15 @@ def tile_moe_two_glu_relu_kernel(
         load_scales(s1[:], w1_scales)
         load_scales(s3[0][:], w3_scales[:PAIR])
         load_raw(w3[0][:], w3_words[0, 0])
-        for e in range(1, LAST):
+        for e in range(1, E):
             load_raw(w1[e][:], w1_words[e, 0])
             if e == PAIR:
                 load_scales(s3[1][:], w3_scales[PAIR:])
             load_raw(w3[e][:], w3_words[e, 0])
-        load_raw(w1[LAST][:], w1_words[LAST, 0])
-        load_last_half(0)
         load_scales(s2[:], w2_scales)
-        load_second(w2_early[0], 0, 1)
-        load_last_half(1)
-        load_second(w2_early[1], 1, 1)
         nc.sync.dma_start(places[:], dst)
-        load_second(w2_late, PAIR, PAIR)
+        for q in range(E // PAIR):
+            load_second(q)
 
         spread = banks[GATE_BANK][:].rearrange("n (u p) -> n u p", u=PACK)
         for u in range(PACK):
@@ -170,18 +162,19 @@ def tile_moe_two_glu_relu_kernel(
                     quantise_tokens(e - 1)
         quantise_tokens(LAST)
 
-        gates = keep.tile([P, E * C], F32, name="gates")
+        gates = keep.tile([P, E * C], F32, name="gates", tag="plane%d" % (PACK - 1))
         nc.vector.tensor_copy(gates[:].rearrange("n (p u) -> n p u", u=PACK), spread.rearrange("n u p -> n p u"))
 
         relus = per_half("relu", F32)
         hidden = per_half("hidden", BF16)
-        turned = per_expert("turned", [P, PASSES * C * PACK], BF16)
+        turned = per_expert("turned", [P, PASSES * C * PACK], BF16, range(PAIR))
+        turned_halves = [per_expert("turned%d_" % e, [P, C * PACK], BF16, range(PASSES)) for e in range(PAIR, E)]
         code_tags = ["hidden_codes0", "relu2_0", "hidden_codes2", "hidden_codes3"]
         hidden_codes = [
             keep.tile([P, PASSES * C], U32, name="hidden_codes%d" % e, align_bytes=64, tag=code_tags[e]) for e in range(E)
         ]
         hidden_scales = per_expert("hidden_scales", [P, PASSES * C], U8)
-        gated = per_expert("gated", [P, C], F32)
+        y_copies = per_expert("y_copy", [P, C], F32)
 
         def multiply_first(e, g, bank, words, scales):
             nc.tensor.matmul_mx(
@@ -198,7 +191,7 @@ def tile_moe_two_glu_relu_kernel(
             multiply_first(e, g, A_BANKS[e][g], w1[e][:, 2 * g * HALF : 2 * (g + 1) * HALF], s1[:, e, :])
 
         def multiply_b(e, g):
-            words = w3_last[g][:] if e == LAST else w3[e][:, 2 * g * HALF : 2 * (g + 1) * HALF]
+            words = w3[e][:, 2 * g * HALF : 2 * (g + 1) * HALF]
             multiply_first(e, g, B_BANKS[e][g], words, s3[e // PAIR][:, e % PAIR, :])
 
         def bank_order(bank):
@@ -232,30 +225,40 @@ def tile_moe_two_glu_relu_kernel(
 
         def empty_half(e, g):
             bank, side = TURNED_PLACES[e][g]
-            copy = nc.scalar.copy if g == 0 else nc.vector.tensor_copy
-            copy(turned_words(e)[:, g], sides(bank)[:, side].rearrange("p v c -> p c v"))
+            words = turned_halves[e - PAIR][g][:].bitcast(F32).rearrange("p (c v) -> p c v", v=2)
+            nc.scalar.copy(words, sides(bank)[:, side].rearrange("p v c -> p c v"))
+
+        def quantise_half(e, g):
+            nc.vector.quantize_mx(
+                out=hidden_codes[e][:, g * C : (g + 1) * C].bitcast(FP8X4),
+                scales=hidden_scales[e][:, g * C : (g + 1) * C],
+                in_=turned_halves[e - PAIR][g][:],
+            )
 
         def quantise_hidden(e):
             nc.vector.quantize_mx(out=hidden_codes[e][:].bitcast(FP8X4), scales=hidden_scales[e][:], in_=turned[e][:])
 
         def multiply_second(e):
-            for g in range(PASSES):
-                words = w2_early[e][:, g, :] if e < PAIR else w2_late[:, (e - PAIR) * PASSES + g, :]
+            order = list(reversed(range(PASSES))) if e == 2 else list(range(PASSES))
+            for g in order:
+                words = w2[e // PAIR][:, (e % PAIR) * PASSES + g, :]
                 nc.tensor.matmul_mx(
                     out=banks[Y_BANKS[e]][:, :C],
                     lhsT=words.bitcast(FP4X4),
                     lhsT_scale=s2[:, e * PASSES + g, :],
                     rhs=hidden_codes[e][:, g * C : (g + 1) * C].bitcast(FP8X4),
                     rhs_scale=hidden_scales[e][:, g * C : (g + 1) * C],
-                    start=(g == 0),
-                    stop=(g == PASSES - 1),
+                    start=(g == order[0]),
+                    stop=(g == order[-1]),
                 )
 
         def take_out(e):
-            nc.vector.tensor_tensor(gated[e][:], banks[Y_BANKS[e]][:, :C], gates[:, e * C : (e + 1) * C], MULT)
+            nc.scalar.copy(y_copies[e][:], banks[Y_BANKS[e]][:, :C])
 
         def send_back(e):
-            nc.scalar.activation(result[:].indirect(slots_of(places, e)), gated[e][:], COPY)
+            nc.vector.tensor_tensor(
+                result[:].indirect(slots_of(places, e)), y_copies[e][:], gates[:, e * C : (e + 1) * C], MULT
+            )
 
         def first_layer(e):
             for call in (multiply_a, multiply_b, rectify, gate_hidden):
@@ -268,35 +271,27 @@ def tile_moe_two_glu_relu_kernel(
             empty_both(e)
             quantise_hidden(e)
 
+        def half_to_codes(e, g):
+            turn(e, g)
+            empty_half(e, g)
+            quantise_half(e, g)
+
         first_layer(0)
         first_layer(1)
         to_codes(0)
         first_layer(2)
         to_codes(1)
-        for g in range(PASSES):
-            multiply_a(LAST, g)
-        multiply_b(LAST, 0)
-        for g in range(PASSES):
-            rectify(LAST, g)
-        gate_hidden(LAST, 0)
+        first_layer(LAST)
+        half_to_codes(2, 1)
         multiply_second(0)
-        turn(2, 0)
         take_out(0)
-        empty_half(2, 0)
         send_back(0)
-        multiply_b(LAST, 1)
-        gate_hidden(LAST, 1)
         multiply_second(1)
-        turn(2, 1)
-        empty_half(2, 1)
+        half_to_codes(2, 0)
         take_out(1)
-        quantise_hidden(2)
-        turn(LAST, 0)
-        empty_half(LAST, 0)
+        half_to_codes(LAST, 0)
         send_back(1)
-        turn(LAST, 1)
-        empty_half(LAST, 1)
-        quantise_hidden(LAST)
+        half_to_codes(LAST, 1)
         for e in range(PAIR, E):
             multiply_second(e)
             take_out(e)

@@ -56,8 +56,7 @@ def tile_moe_two_glu_relu_kernel(
         planes = [keep.tile([P, T], F32, name="plane%d" % t, tag="plane%d" % t) for t in range(PACK)]
         gate_row = keep.tile([P, PACK], F32, name="gate_row")
         w1 = per_expert("w1_", [P, 2 * H], U8)
-        w3_tags = ["w3_0", "w3_1", "w3_0", "w3_3"]
-        w3 = [keep.tile([P, 2 * H], U8, name="w3_%d" % e, tag=w3_tags[e], align_bytes=64) for e in range(E)]
+        w3 = per_expert("w3_", [P, 2 * H], U8)
         w2 = per_expert("w2_", [P, PAIR * PASSES, 2 * N], U8, range(E // PAIR))
         s1 = keep.tile([P, E, H], U8, name="s1", align_bytes=64)
         s3 = per_expert("s3_", [P, PAIR, H], U8, range(E // PAIR))

from contextlib import ExitStack

import concourse.mybir as mybir
from concourse.masks import make_identity

K, T, E, C, H, N = 512, 1024, 4, 128, 1024, 128
P = 128
FLOPS = 2 * E * C * (2 * K * H + H * N)

F32 = mybir.dt.float32
BF16 = mybir.dt.bfloat16
I32 = mybir.dt.int32
U32 = mybir.dt.uint32
U16 = mybir.dt.uint16
U8 = mybir.dt.uint8
FP8X4 = mybir.dt.float8_e4m3fn_x4
FP4X4 = mybir.dt.float4_e2m1fn_x4
MULT = mybir.AluOpType.mult
RELU = mybir.ActivationFunctionType.Relu
COPY = mybir.ActivationFunctionType.Copy

PACK = 4
HALF = 512
PASSES = H // HALF
SCALE_ROWS = 16
LIST_COLS = C // 16
PAIR = 2
LAST = E - 1
WARM_UP_PASSES = 2

A_BANKS = ((0, 1), (4, 5), (0, 1), (0, 1))
B_BANKS = ((2, 3), (6, 7), (2, 3), (6, 7))
Y_BANKS = (2, 3, 4, 5)
TURNED_PLACES = (((4, 0), (4, 1)), ((5, 0), (5, 1)), ((3, 1), (0, 1)), ((2, 0), (3, 1)))
WARM_UP_BANK, GATE_BANK = B_BANKS[1]


def tile_moe_two_glu_relu_kernel(
    tc, xT, w1_words, w1_scales, w3_words, w3_scales, w2_words, w2_scales, gate, offs, dst, out
):
    nc = tc.nc
    with ExitStack() as ctx:
        keep = ctx.enter_context(tc.tile_pool(name="keep", bufs=1))
        psum = ctx.enter_context(tc.psum_pool(name="psum", bufs=1))
        banks = [psum.tile([P, HALF], F32, name="bank%d" % n) for n in range(8)]

        def per_expert(name, shape, dtype, experts=range(E)):
            return [keep.tile(shape, dtype, name="%s%d" % (name, e), align_bytes=64) for e in experts]

        def per_half(name, dtype):
            names = [["%s%d_%d" % (name, e, g) for g in range(PASSES)] for e in range(E)]
            return [[keep.tile([P, HALF], dtype, name=n, tag=n, align_bytes=64) for n in row] for row in names]

        sources = keep.tile([P, E * LIST_COLS], U16, name="sources")
        places = keep.tile([P, E * LIST_COLS], U16, name="places")
        planes = [keep.tile([P, T], F32, name="plane%d" % t, tag="plane%d" % t) for t in range(PACK)]
        gate_row = keep.tile([P, PACK], F32, name="gate_row")
        w1 = per_expert("w1_", [P, 2 * H], U8)
        w3 = per_expert("w3_", [P, 2 * H], U8)
        w2 = per_expert("w2_", [P, PAIR * PASSES, 2 * N], U8, range(E // PAIR))
        s1 = keep.tile([P, E, H], U8, name="s1", align_bytes=64)
        s3 = per_expert("s3_", [P, PAIR, H], U8, range(E // PAIR))
        s2 = keep.tile([P, E * PASSES, N], U8, name="s2", align_bytes=64)
        identity = keep.tile([P, P], F32, name="identity")

        column = keep.tile([P, 1], F32, name="column")
        nc.vector.memset(column[:], 0.0)
        result = keep.tile([P, T], F32, name="result")
        nc.scalar.activation(result[:], column[:].to_broadcast([P, T]), RELU)
        for scales in (s1, s3[0], s3[1], s2):
            nc.vector.memset(scales[:].bitcast(I32), 0)
        make_identity(nc, identity[:])

        def load_plane(t):
            nc.sync.dma_start(planes[t][:], xT.rearrange("(p t) n -> p t n", t=PACK)[:, t, :])

        def load_raw(into, source):
            nc.sync.dma_start(into.bitcast(I32), source.bitcast(I32))

        def load_scales(into, rows):
            rows = rows.bitcast(I32).rearrange("e s q c -> q (e s) c")
            for r in range(4):
                nc.sync.dma_start(into.bitcast(I32)[r:P:32, :, :], rows[r:SCALE_ROWS:4, :, :])

        def load_second(q):
            words = w2_words[q * PAIR : (q + 1) * PAIR].bitcast(I32).rearrange("e s p c -> p (e s) c")
            nc.sync.dma_start(w2[q][:].bitcast(I32), words)

        load_plane(0)
        nc.sync.dma_start(sources[:], offs)
        nc.sync.dma_start(gate_row[:], gate[0].rearrange("(p u) -> p u", u=PACK))
        load_plane(2)
        load_plane(1)
        load_plane(3)
        load_raw(w1[0][:], w1_words[0, 0])
        load_scales(s1[:], w1_scales)
        load_scales(s3[0][:], w3_scales[:PAIR])
        load_raw(w3[0][:], w3_words[0, 0])
        for e in range(1, E):
            load_raw(w1[e][:], w1_words[e, 0])
            if e == PAIR:
                load_scales(s3[1][:], w3_scales[PAIR:])
            load_raw(w3[e][:], w3_words[e, 0])
        load_scales(s2[:], w2_scales)
        nc.sync.dma_start(places[:], dst)
        for q in range(E // PAIR):
            load_second(q)

        spread = banks[GATE_BANK][:].rearrange("n (u p) -> n u p", u=PACK)
        for u in range(PACK):
            nc.tensor.transpose(spread[:, u, :], gate_row[:, u : u + 1].to_broadcast([P, P]), identity[:])

        rounded = [keep.tile([P, T], BF16, name="rounded%d" % t, align_bytes=64) for t in range(2)]
        tokens = per_expert("tokens", [P, C, PACK], BF16)
        token_codes = per_expert("token_codes", [P, C], U32)
        token_scales = per_expert("token_scales", [P, C], U8)

        def slots_of(offsets, e):
            return offsets[:, e * LIST_COLS : (e + 1) * LIST_COLS]

        def quantise_tokens(e):
            nc.vector.quantize_mx(
                out=token_codes[e][:].bitcast(FP8X4),
                scales=token_scales[e][:],
                in_=tokens[e][:].rearrange("p c t -> p (c t)"),
            )

        idle_codes = keep.tile([P, HALF], U32, name="idle_codes", align_bytes=64)
        idle_scales = keep.tile([P, HALF], U8, name="idle_scales", align_bytes=64)

        def warm_up():
            width = T // PACK
            for start in range(0, HALF, width):
                nc.vector.quantize_mx(
                    out=idle_codes[:, start : start + width].bitcast(FP8X4),
                    scales=idle_scales[:, start : start + width],
                    in_=rounded[0][:],
                )
            for repeat in range(WARM_UP_PASSES):
                nc.tensor.matmul_mx(
                    out=banks[WARM_UP_BANK][:],
                    lhsT=w1[0][:, : 2 * P].bitcast(FP4X4),
                    lhsT_scale=idle_scales[:, :P],
                    rhs=idle_codes[:].bitcast(FP8X4),
                    rhs_scale=idle_scales[:],
                    start=True,
                    stop=True,
                )

        for t in range(2):
            if t == 0:
                nc.vector.tensor_copy(rounded[t][:], planes[t][:])
                warm_up()
            else:
                nc.scalar.activation(rounded[t][:], planes[t][:], COPY)
            for e in range(E):
                nc.scalar.activation(tokens[e][:, :, t], rounded[t][:].indirect(slots_of(sources, e)), COPY)
            for e in range(E):
                nc.vector.tensor_copy(tokens[e][:, :, t + 2], planes[t + 2][:].indirect(slots_of(sources, e)))
                if t == 1 and e > 0:
                    quantise_tokens(e - 1)
        quantise_tokens(LAST)

        gates = keep.tile([P, E * C], F32, name="gates", tag="plane%d" % (PACK - 1))
        nc.vector.tensor_copy(gates[:].rearrange("n (p u) -> n p u", u=PACK), spread.rearrange("n u p -> n p u"))

        relus = per_half("relu", F32)
        hidden = per_half("hidden", BF16)
        turned = per_expert("turned", [P, PASSES * C * PACK], BF16, range(PAIR))
        turned_halves = [per_expert("turned%d_" % e, [P, C * PACK], BF16, range(PASSES)) for e in range(PAIR, E)]
        code_tags = ["hidden_codes0", "relu2_0", "hidden_codes2", "hidden_codes3"]
        hidden_codes = [
            keep.tile([P, PASSES * C], U32, name="hidden_codes%d" % e, align_bytes=64, tag=code_tags[e]) for e in range(E)
        ]
        hidden_scales = per_expert("hidden_scales", [P, PASSES * C], U8)
        y_copies = per_expert("y_copy", [P, C], F32)

        def multiply_first(e, g, bank, words, scales):
            nc.tensor.matmul_mx(
                out=banks[bank][:],
                lhsT=token_codes[e][:].bitcast(FP8X4),
                lhsT_scale=token_scales[e][:],
                rhs=words.bitcast(FP4X4),
                rhs_scale=scales[:, g * HALF : (g + 1) * HALF],
                start=True,
                stop=True,
            )

        def multiply_a(e, g):
            multiply_first(e, g, A_BANKS[e][g], w1[e][:, 2 * g * HALF : 2 * (g + 1) * HALF], s1[:, e, :])

        def multiply_b(e, g):
            words = w3[e][:, 2 * g * HALF : 2 * (g + 1) * HALF]
            multiply_first(e, g, B_BANKS[e][g], words, s3[e // PAIR][:, e % PAIR, :])

        def bank_order(bank):
            return bank[:].rearrange("s (m v d) -> s v m d", v=2, d=2)

        def pair_order(tile):
            return tile[:].rearrange("s (v m d) -> s v m d", v=2, d=2)

        def rectify(e, g):
            nc.scalar.activation(pair_order(relus[e][g]), bank_order(banks[A_BANKS[e][g]]), RELU)

        def gate_hidden(e, g):
            nc.vector.tensor_tensor(
                pair_order(hidden[e][g]), bank_order(banks[B_BANKS[e][g]]), pair_order(relus[e][g]), MULT
            )

        def sides(bank):
            return banks[bank][:].rearrange("p (side v c) -> p side v c", side=2, v=2)

        def turn(e, g):
            bank, side = TURNED_PLACES[e][g]
            pairs = hidden[e][g][:].bitcast(F32)
            for v in range(2):
                nc.tensor.transpose(sides(bank)[:, side, v, :], pairs[:, v * P : (v + 1) * P], identity[:])

        def turned_words(e):
            return turned[e][:].bitcast(F32).rearrange("p (g c v) -> p g c v", g=PASSES, v=2)

        def empty_both(e):
            nc.scalar.copy(turned_words(e), sides(TURNED_PLACES[e][0][0]).rearrange("p g v c -> p g c v"))

        def empty_half(e, g):
            bank, side = TURNED_PLACES[e][g]
            words = turned_halves[e - PAIR][g][:].bitcast(F32).rearrange("p (c v) -> p c v", v=2)
            nc.scalar.copy(words, sides(bank)[:, side].rearrange("p v c -> p c v"))

        def quantise_half(e, g):
            nc.vector.quantize_mx(
                out=hidden_codes[e][:, g * C : (g + 1) * C].bitcast(FP8X4),
                scales=hidden_scales[e][:, g * C : (g + 1) * C],
                in_=turned_halves[e - PAIR][g][:],
            )

        def quantise_hidden(e):
            nc.vector.quantize_mx(out=hidden_codes[e][:].bitcast(FP8X4), scales=hidden_scales[e][:], in_=turned[e][:])

        def multiply_second(e):
            order = list(reversed(range(PASSES))) if e == 2 else list(range(PASSES))
            for g in order:
                words = w2[e // PAIR][:, (e % PAIR) * PASSES + g, :]
                nc.tensor.matmul_mx(
                    out=banks[Y_BANKS[e]][:, :C],
                    lhsT=words.bitcast(FP4X4),
                    lhsT_scale=s2[:, e * PASSES + g, :],
                    rhs=hidden_codes[e][:, g * C : (g + 1) * C].bitcast(FP8X4),
                    rhs_scale=hidden_scales[e][:, g * C : (g + 1) * C],
                    start=(g == order[0]),
                    stop=(g == order[-1]),
                )

        def take_out(e):
            nc.scalar.copy(y_copies[e][:], banks[Y_BANKS[e]][:, :C])

        def send_back(e):
            nc.vector.tensor_tensor(
                result[:].indirect(slots_of(places, e)), y_copies[e][:], gates[:, e * C : (e + 1) * C], MULT
            )

        def first_layer(e):
            for call in (multiply_a, multiply_b, rectify, gate_hidden):
                for g in range(PASSES):
                    call(e, g)

        def to_codes(e):
            for g in range(PASSES):
                turn(e, g)
            empty_both(e)
            quantise_hidden(e)

        def half_to_codes(e, g):
            turn(e, g)
            empty_half(e, g)
            quantise_half(e, g)

        first_layer(0)
        first_layer(1)
        to_codes(0)
        first_layer(2)
        to_codes(1)
        first_layer(LAST)
        half_to_codes(2, 1)
        multiply_second(0)
        take_out(0)
        send_back(0)
        multiply_second(1)
        half_to_codes(2, 0)
        take_out(1)
        half_to_codes(LAST, 0)
        send_back(1)
        half_to_codes(LAST, 1)
        for e in range(PAIR, E):
            multiply_second(e)
            take_out(e)
            send_back(e)
        nc.sync.dma_start(out, result[:])
